import numpy as np, ml_dtypes
CORES = [8,136,40,168]
N = 4
BF = ml_dtypes.bfloat16
W, I, D, T = 2048, 128, 3, 6
B = W // I
def basic(rng):
    return (rng.integers(0, 256, (N, 8, 16, W)), rng.integers(0, W, (N, 8, 16, I)), rng.integers(0, D, (N, 8, 16, I)), rng.integers(0, W, (N, 8, 16, I, D)),
            rng.integers(0, 16, (N, 8, 16)), rng.integers(800, 1151, (N, 8, 16)))
def some(rng, a):
    return np.argsort(rng.random((N, 8, 16, I)), axis=2) < a[:, :, None, :]
def seat(rng, on):
    place = np.argsort(rng.random((N, 8, 16, I)), axis=2)
    near = place + rng.integers(0, 225, (N, 8, 1, I)); far = 15 * place + rng.integers(0, 15, (N, 8, 16, I))
    return np.where(on, np.where(rng.random((N, 8, 1, I)) < 0.5, near, far), -1)
def blame(rng, on, free_, dead):
    o = on.astype(np.int64); order = np.argsort(np.where(on, 0.0, 2.0) + rng.random(on.shape), axis=2); loc = np.argsort(order, axis=2)[..., None]
    cnt = (np.add.reduce(o, axis=2)[:, :, None, :] - o)[..., None]
    m = (rng.random((N, 8, 16, I, D)) * cnt).astype(np.int64); m = np.where(on[..., None] & (m >= loc), m + 1, m)
    who = np.take_along_axis(order[..., None], np.minimum(m, 15), axis=2); who = np.where(cnt > 0, who, -1)
    u = rng.random((N, 8, 16, I, D))
    return np.where(u < free_, -1, np.where(u < free_ + dead, -2, who))
def pack(x, n, q, v, e, c, w, t):
    return {"xt": x.reshape(N, 128, W).astype(BF), "nm": n.reshape(N, 128, I).astype(np.int32), "ps": q.reshape(N, 128, I).astype(BF), "dv": v.reshape(N, 128, I).astype(BF),
            "ex": e.reshape(N, 128, I * D).astype(BF), "dn": c.reshape(N, 128, I * D).astype(np.int32), "wt": w.reshape(N, 128, 1).astype(np.int32), "th": t.reshape(N, 128, 1).astype(np.int32)}
def setup_inputs(rng):
    x, n, v, c, w, t = basic(rng); on = some(rng, rng.integers(0, 17, (N, 8, I)))
    return pack(x, n, seat(rng, on), v, blame(rng, on, rng.choice(np.array([0.03, 0.1, 0.3, 0.7]), (N, 8, 1, I, 1)), 0.1), c, w, t)
def setup_inputs_spread(rng):
    x, n, v, c, w, t = basic(rng)
    x = np.floor(rng.random((N, 8, 16, W)) * np.exp2(rng.integers(0, 9, (N, 8, 1, W)))).astype(np.int64)
    n = (W * rng.random((N, 8, 16, I)) ** 3).astype(np.int64); c = (W * rng.random((N, 8, 16, I, D)) ** 2).astype(np.int64)
    t = np.minimum(np.exp2(12 * rng.random((N, 8, 16))).astype(np.int64) - 1, 4080)
    on = some(rng, (17 * rng.random((N, 8, I)) ** 2).astype(np.int64))
    return pack(x, n, seat(rng, on), v, blame(rng, on, rng.choice(np.array([0.0, 0.2, 0.6]), (N, 8, 1, I, 1)), 0.15), c, w, t)
def setup_inputs_ends(rng):
    x, n, v, c, w, t = basic(rng)
    kind = rng.integers(0, 4, (N, 8, 1, W)); x = np.where(kind == 0, 0, np.where(kind == 1, 255, 255 * rng.integers(0, 2, (N, 8, 16, W))))
    x[..., 0] = 0; x[..., W - 1] = 255; x[..., W - 37] = 0; x[:, ::2, :, W - W // 16 - 38] = 255; x[:, 1::2, :, W - W // 16 - 38] = 0
    x[:, 3, :, W - 37] = np.where(np.argsort(rng.random((N, 16)), axis=1) < 9, 0, 255)
    x[:, 3, :, W - W // 16 - 38] = np.where(np.argsort(rng.random((N, 16)), axis=1) < 11, 0, 255)
    x[:, 5, :, W - 37] = 255
    n = np.where(rng.random(n.shape) < 0.85, (W - 1) * rng.integers(0, 2, n.shape), n); c = np.where(rng.random(c.shape) < 0.85, (W - 1) * rng.integers(0, 2, c.shape), c)
    v = (D - 1) * rng.integers(0, 2, v.shape); w = 15 * rng.integers(0, 2, w.shape); w[:, 7] = 15; w[:, 0, 0] = 0
    z = np.array([0, 4080, 4079, 1])
    t[:, ::2] = rng.choice(z, (N, 4, 16), p=[0.85, 0.05, 0.05, 0.05]); t[:, 1::2] = rng.choice(z, (N, 4, 16), p=[0.3, 0.5, 0.1, 0.1])
    t[:, 7] = 4079; t[:, 7, 5] = 4080; t[:, 7, 14] = 4080; t[:, 5] = 0; t[:, 3] = rng.choice(np.array([2295, 2804]), (N, 16))
    on = some(rng, rng.choice(np.array([0, 1, 2, 4, 8, 15, 16]), (N, 8, I))); on[:, :, 15] |= rng.random((N, 8, I)) < 0.85
    on[:, 7, :, I - 1] = True; on[:, 7, 15, I - 1] = False
    on[:, 7, :, I - 2] = True
    for k in (5, 14, 15): on[:, 7, k, I - 2] = False
    climb = (0, I // 2, (W - W // 16 - 38) // B, (W - 37) // B, I - 1)
    crest = (1, I // 2 + 1, (W - 37) // B - 1)
    for i in climb + crest: on[:, 5, :, i] = False; on[:, 5, 15, i] = True
    place = np.argsort(rng.random((N, 8, 16, I)), axis=2); q = np.where(on, np.where(place < 8, place, 224 + place), -1)
    kk = np.arange(16).reshape(1, 1, 16, 1, 1); u = rng.random((N, 8, 16, I, D)); b = blame(rng, on, 0.5, 0.0)
    hot = np.where(u < 0.4, 15, np.where(u < 0.75, -2, np.where(u < 0.9, -1, b))); calm = np.where(u < 0.7, -2, np.where(u < 0.85, -1, b))
    e = np.where(on[:, :, 15][:, :, None, :, None] & (kk != 15), hot, calm)
    e[:, 7, 15, I - 1] = -1; c[:, 7, 15, I - 1] = W - 1; n[:, 7, 0:15:2, I - 1] = 0; n[:, 7, 1:15:2, I - 1] = W - 1
    e[:, 7, 5, I - 2] = -1; c[:, 7, 5, I - 2] = 0; n[:, 7, :, I - 2] = W - 1
    for i in climb + crest: q[:, 5, 15, i] = 239; e[:, 5, :, i] = -1; n[:, 5, :, i] = W - 1; c[:, 5, :, i] = W - 1
    for i in crest: c[:, 5, T - 2, i] = 0
    return pack(x, n, q, v, e, c, w, t)
def setup_inputs_corners(rng):
    x, n, v, c, w, t = basic(rng)
    x = 32 * rng.integers(0, 8, (N, 8, 16, W)); t = 32 * rng.integers(26, 36, (N, 8, 16)) - rng.integers(0, 2, (N, 8, 16))
    t = np.where(rng.random(t.shape) < 0.08, rng.choice(np.array([0, 4080]), t.shape), t); w = rng.choice(np.array([0, 1, 15]), w.shape)
    n = np.where(rng.random(n.shape) < 0.05, 0, n); c = np.where(rng.random(c.shape) < 0.05, 0, c)
    a = rng.choice(np.array([0, 1, 2, 15, 16]), (N, 8, I)); a[:, 3] = 16; a[1::2, 3, I - 1] = 15
    on = some(rng, a); q = seat(rng, on)
    full = blame(rng, on, 0.0, 0.0); mix = blame(rng, on, 0.0, 0.6); last = full.copy(); last[..., D - 1] = -1
    kk = np.arange(16).reshape(1, 1, 16, 1, 1); j = np.argmax(q, axis=2)[:, :, None, :, None]; some_on = np.any(on, axis=2)[:, :, None, :, None]
    top = np.where((kk != j) & some_on, j, -2); m = rng.integers(0, 7, (N, 8, 1, I, 1))
    e = np.where(m == 0, -1, np.where(m == 1, -2, np.where(m == 2, full, np.where(m == 3, last, np.where(m == 4, full[..., :1], np.where(m == 5, mix, top))))))
    e = np.where(m >= 0, e, np.zeros((N, 8, 16, I, D), np.int64))
    return pack(x, n, q, v, e, c, w, t)
def setup_inputs_crowd(rng):
    x, n, v, c, w, t = basic(rng)
    on = some(rng, rng.choice(np.array([1, 2, 8, 14, 15]), (N, 8, I))); q = seat(rng, on)
    kk = np.arange(16).reshape(1, 1, 16, 1, 1); j = np.argmax(q, axis=2)[:, :, None, :, None]
    own = blame(rng, on, 0.3, 0.1); other = blame(rng, on, 0.0, 0.2)
    own[:, 5] = -1; own[1::2, 5, :, 0] = -2
    e = np.where(kk == j, own, j); alt = np.where(kk == j, own, other); e[:, 1::2, :, :, D - 1] = alt[:, 1::2, :, :, D - 1]
    p = np.argmax(q < 0, axis=2)
    for r in range(1, N, 2): e[r, 7, p[r, 7, I - 1], I - 1, 0] = -1
    t[:, ::3] = 4080; t[:, 1::3] = 4080; t[:, 1::3, 5] = 0; t[:, 5] = 0
    n[:, 0:2] = n[:, 0:2, :1].copy(); c[:, 2] = c[:, 2, :1, :, :1].copy()
    n[:, 5] = (W // 2) * rng.integers(0, 2, (N, 16, I)); c[:, 5] = np.where(c[:, 5] % (W // 8) == 0, c[:, 5] + 1, c[:, 5])
    return pack(x, n, q, v, e, c, w, t)
def setup_inputs_few(rng):
    x, n, v, c, w, t = basic(rng); on = some(rng, rng.integers(0, 17, (N, 8, I))); chains = []
    for r in range(N):
        for g in rng.permutation(8)[:r % 4]:
            i = (0, I - 1, int(rng.integers(0, I)))[int(rng.integers(0, 3))]; on[r, g, :, i] = True; on[r, g, int(rng.integers(0, 16)), i] = False
            chains.append((r, int(g), i, T if r < 4 else int(rng.integers(1, T + 1))))
    q = seat(rng, on); e = np.where(on[..., None], blame(rng, on, 0.2, 0.2), -1)
    for r, g, i, k in chains:
        o = np.argsort(-q[r, g, :, i])
        e[r, g, :, i] = -1; e[r, g, o[15], i] = o[0]
        for m in range(k - 1): e[r, g, o[m], i] = o[m + 1]
    return pack(x, n, q, v, e, c, w, t)
def check_inputs(d):
    bad = []
    for k, lo, hi in (("xt", 0, 255), ("nm", 0, W - 1), ("ps", -1, 239), ("dv", 0, D - 1), ("ex", -2, 15), ("dn", 0, W - 1), ("wt", 0, 15), ("th", 0, 4080)):
        v = np.asarray(d[k]).astype(np.float64)
        if not (np.min(v) >= lo and np.max(v) <= hi and np.all(v == np.floor(v))): bad.append("range of " + k)
    if not bad:
        q = d["ps"].astype(np.int64).reshape(N, 8, 16, I); e = d["ex"].astype(np.int64).reshape(N, 8, 16, I, D); s = np.sort(q, axis=2)
        if np.any((s[:, :, 1:] == s[:, :, :-1]) & (s[:, :, 1:] >= 0)): bad.append("equal places in a puzzle of ps")
        if np.any(e == np.arange(16).reshape(1, 1, 16, 1, 1)): bad.append("a variable is its own culprit in ex")
        if np.any((e >= 0) & (np.take_along_axis(q[..., None], np.maximum(e, 0), axis=2) < 0)): bad.append("an unassigned culprit in ex")
    return bad
def reference(xt, nm, ps, dv, ex, dn, wt, th):
    X = xt.astype(np.int32).reshape(N, 8, 16, W); names = nm.astype(np.int64).reshape(N, 8, 16, I); place = ps.astype(np.int64).reshape(N, 8, 16, I)
    value = dv.astype(np.int64).reshape(N, 8, 16, I); expl = ex.astype(np.int64).reshape(N, 8, 16, I, D); dom = dn.astype(np.int64).reshape(N, 8, 16, I, D)
    w = wt.astype(np.int64).reshape(N, 8, 16, 1); thr = th.astype(np.int64).reshape(N, 8, 16, 1)
    pend = np.full((N, 8, I), -1, np.int64); A = [0] * N
    gi = np.arange(8)[:, None]; ii = np.arange(I)[None, :]; rows = np.arange(16)[None, :, None]
    for t in range(T):
        cuts = [0] * N
        for r in range(N):
            s = (r + t) % N
            n, q, v, e, pe, xs = names[r], place[r], value[r], expl[r], pend[r], X[s]
            full = np.all(q >= 0, axis=1); o = np.argmin(q, axis=1)
            p = np.where(pe >= 0, pe, np.where(full, o, np.argmax(q < 0, axis=1)))
            out = full[:, None, :] & (rows == o[:, None, :])
            q[out] = -1; e[out] = -1; e[full[:, None, :, None] & (e == o[:, None, :, None])] = -1
            mine = e[gi, p, ii]
            none = np.all(mine == -2, axis=2); cut = np.all(mine != -1, axis=2) & ~none
            e[(rows == p[:, None, :]) & none[:, None, :]] = -1
            key = np.where(np.any(mine[:, None] == rows[..., None], axis=3), q, -1); j = np.argmax(key, axis=1)
            key = np.where(rows == j[:, None, :], -1, key); j2 = np.where(np.max(key, axis=1) >= 0, np.argmax(key, axis=1), -2)
            g1, i1 = np.nonzero(cut); jj = j[cut]
            e[g1, jj, i1, v[g1, jj, i1]] = j2[cut]
            e[cut[:, None, :, None] & (e == j[:, None, :, None])] = -1
            q[g1, jj, i1] = -1; pe[cut] = jj; p = np.where(cut, j, p); cuts[r] = int(np.count_nonzero(cut))
            free_ = e[gi, p, ii] == -1; has = np.any(free_, axis=2); d = np.argmax(free_, axis=2); c = dom[s][gi, p, ii, d]
            cc = c[:, None, :]; at = ((n * cc >> 5) + n + 37 * cc) & (W - 1)
            xc = np.take_along_axis(xs, cc, 2); y = np.take_along_axis(xs, at.reshape(8, 1, 16 * I), 2).reshape(8, 16, 16, I)
            on = q >= 0
            clash = on & (np.add.reduce(np.abs(y - xc[:, :, None, :]), axis=1) <= thr[s] + 32 * (A[r] & 7)); hit = np.any(clash, axis=1)
            bad = has & hit; g1, i1 = np.nonzero(bad)
            e[g1, p[bad], i1, d[bad]] = np.argmin(np.where(clash, q, 1000), axis=1)[bad]
            ok = has & ~hit; g1, i1 = np.nonzero(ok); pp = p[ok]
            big = np.max(np.where(on[:, None], y, 0), axis=2); h = np.add.reduce(w[s] * big, axis=1) & (B - 1)
            young = np.max(q, axis=1) + 1
            n[g1, pp, i1] = c[ok]; v[g1, pp, i1] = d[ok]; q[g1, pp, i1] = young[ok]; pe[ok] = -1
            xs[g1, :, B * i1 + h[ok]] = ((xc + big) >> 1)[g1, :, i1]
        A = cuts
    shown = np.where(pend[:, :, None, :] == rows[None], -2, place)
    here = [(s - T + 1) % N for s in range(N)]
    return {"yn": names[here].reshape(N, 128, I).astype(np.float32), "yp": shown[here].reshape(N, 128, I).astype(BF), "yd": value[here].reshape(N, 128, I).astype(BF),
            "yg": expl[here].reshape(N, 128, I * D).astype(BF), "yx": X.reshape(N, 128, W).astype(BF)}

@@ -1,0 +1,709 @@
+from concourse.mybir import AluOpType, ActivationFunctionType
+
+HW = 64
+NV = 6
+ROT = 1184
+LB, LF = 320, 68
+SCRATCH = {
+    "cb": ("sbuf", [128, 12288], "bfloat16"),
+    "cf": ("sbuf", [128, 1024], "float32"),
+    "tb": ("sbuf", [128, 12288], "bfloat16"),
+    "tf": ("sbuf", [128, 2048], "float32"),
+    "ti": ("sbuf", [128, 2048], "int32"),
+    "tu": ("sbuf", [128, 256], "uint16"),
+    "xw": ("sbuf", [128, 4112], "bfloat16"),
+    "lb": ("sbuf", [128, 2 * NV * LB], "bfloat16"),
+    "lf": ("sbuf", [128, 2 * NV * LF], "float32"),
+    "inb": ("sbuf", [128, 640], "bfloat16"),
+    "ini": ("sbuf", [128, 528], "int32"),
+    "ob": ("sbuf", [128, 640], "bfloat16"),
+    "of": ("sbuf", [128, 128], "float32"),
+}
+for _b in range(8):
+    SCRATCH["pb%d" % _b] = ("psum", [128, 512], "float32")
+NDMA = 16
+SEMAPHORES = ["qV", "qS", "qP", "qG", "sent"] + ["arr%d" % i for i in range(4 * (NV - 1))] + ["dma%d" % i for i in range(NDMA)]
+
+AL, AF = AluOpType, ActivationFunctionType
+WIDE = {"float32": 4, "int32": 4, "bfloat16": 2, "uint16": 2}
+PAR = {"cyc": 1.0, "pe": 0.5, "vfix": 30.0, "sfix": 65.0, "same": 60.0, "cross": 100.0, "gat": 1.56, "sca": 3.5,
+       "issue": 1000.0, "flight": 2700.0, "dma": 2200.0, "look": 0.3, "lead": 3000.0, "lead0": 4000.0, "seed": 1, "iters": 1000, "step": 2000.0,
+       "gather": [("S", 0, 18), ("V", 18, 32), ("S", 32, 50), ("V", 50, 64)],
+       "onS": "J2 nq", "turn": 2,
+       "onG": [0.5, -63.5, -4, 192, 2 ** 19, 12, -2, 6, 256, 8, -8, -4096, 8192, -1024] + [16384 * (t - 31) for t in range(NV)]}
+
+
+def tl(buf, a, b, step=1, parts=128):
+    return (buf, a, b, step, parts)
+
+
+def sub(t, a, b, step=1):
+    return (t[0], t[1] + a, t[1] + b, step, t[4])
+
+
+def nel(t):
+    return (t[2] - t[1] + t[3] - 1) // t[3]
+
+
+def width(t):
+    return WIDE[SCRATCH[t[0]][2]]
+
+
+def psum(t):
+    return t[0][:2] == "pb"
+
+
+def build():
+    ops = []
+    top = {}
+    acc = {}
+    lead = [0.0, -1]
+
+    def new(buf, n, parts=128):
+        a = top.get(buf, 0)
+        top[buf] = a + (n + 15) // 16 * 16
+        assert top[buf] <= SCRATCH[buf][1][1], buf
+        return tl(buf, a, a + n, 1, parts)
+
+    def add(eng, kind, args, reads, writes, cost, extra=()):
+        i = len(ops)
+        deps = set(extra)
+        for t in reads:
+            for (a, b, j, w) in acc.get(t[0], []):
+                if w and a < t[2] and t[1] < b:
+                    deps.add(j)
+        for t in writes:
+            for (a, b, j, w) in acc.get(t[0], []):
+                if a < t[2] and t[1] < b:
+                    deps.add(j)
+        for t in writes:
+            if t[3] == 1:
+                acc[t[0]] = [r for r in acc.get(t[0], []) if not (t[1] <= r[0] and r[1] <= t[2])]
+            acc.setdefault(t[0], []).append((t[1], t[2], i, True))
+        for t in reads:
+            acc.setdefault(t[0], []).append((t[1], t[2], i, False))
+        deps.discard(i)
+        banks = set(t[0] for t in list(reads) + list(writes) if psum(t))
+        w0 = (list(writes) + list(reads))[0]
+        role = (kind, w0[0], w0[1] % {"lb": 2 * LB, "lf": 2 * LF}.get(w0[0], 1 << 20), len(reads), lead[0] > 0, lead[1])
+        ops.append({"role": role, "const": w0[0] in ("cb", "cf") or lead[1] < 0, "eng": eng, "kind": kind, "args": args, "deps": deps, "cost": cost, "banks": banks, "lead": lead[0]})
+        return i
+
+    def vcost(n):
+        return max(64.0, n) * PAR["cyc"] + PAR["vfix"]
+
+    def half(*ts_):
+        return 0.5 if all(width(t) == 2 for t in ts_) else 1.0
+
+    def tiles(*xs):
+        return [x for x in xs if isinstance(x, tuple)]
+
+    def ts(out, a, s1, op0, s2=None, op1=None):
+        add("V", "ts", (out, a, s1, s2, op0, op1), tiles(a, s1, s2), [out], vcost(nel(a) * half(out, a)))
+        return out
+
+    def tt(out, a, b, op):
+        c = 1.0 if psum(a) or psum(b) else 2.0 * half(out, a, b)
+        add("V", "tt", (out, a, b, op), [a, b], [out], vcost(nel(a) * c))
+        return out
+
+    def cp(out, a):
+        add("V", "cp", (out, a), [a], [out], vcost(nel(a) * half(out, a)))
+        return out
+
+    def fill(out, v):
+        add("V", "fill", (out, float(v)), [], [out], vcost(nel(out) * half(out)))
+        return out
+
+    def scan(out, d0, d1):
+        add("V", "scan", (out, d0, d1), [d0, d1], [out], vcost(nel(d1) * half(out, d0, d1)))
+        return out
+
+    def act(out, a, fn, bias=0.0, scale=1.0, accum=None, more=0.0):
+        add("S", "act", (out, a, fn, bias, scale, accum), tiles(a, bias, scale), tiles(out, accum),
+            max(64.0, nel(a)) * PAR["cyc"] + PAR["sfix"] + more)
+        return out
+
+    def mm(terms, start=True, stop=True):
+        cost = sum(max(64.0, nel(r)) * (4.0 if width(r) == 4 else 1.0) for (_o, _l, r) in terms) * PAR["pe"] + 30.0
+        rd = [l for (_o, l, _r) in terms] + [r for (_o, _l, r) in terms]
+        wr = [o for (o, _l, _r) in terms]
+        if start != stop:
+            wr.append(tl(wr[0][0], 0, 512))
+        add("P", "mm", (terms, start, stop), rd, wr, cost)
+
+    def gather(eng, out, win, off):
+        add(eng, "gat", (out, win, off), [win, off], [out], nel(out) * PAR["gat"] * PAR["cyc"] + 60.0)
+        return out
+
+    def dma(eng, out, a):
+        add(eng, "dma", (out, a), [a] if a[0] in SCRATCH else [], [out] if out[0] in SCRATCH else [], 100.0)
+
+    def iota(out, pat, base, cm):
+        add("G", "iota", (out, pat, base, cm), [], [out], 130.0 + 2.0 * nel(out))
+        return out
+
+    def select(out, a, pat, op, v, cm):
+        add("G", "sel", (out, a, pat, op, float(v), cm), [a], [out], 170.0 + 2.0 * nel(out))
+        return out
+
+    ps_in, dv_in, ex_in = tl("inb", 0, 128), tl("inb", 128, 256), tl("inb", 256, 640)
+    nm_in, dn_in, wt_in, th_in = tl("ini", 0, 128), tl("ini", 128, 512), tl("ini", 512, 513), tl("ini", 520, 521)
+    lead[0] = 1e6
+    dma("Y", ps_in, tl("ps", 0, 128))
+    dma("S", ex_in, tl("ex", 0, 384))
+    dma("Y", dv_in, tl("dv", 0, 128))
+    dma("S", dn_in, tl("dn", 0, 384))
+    lead[0] = 0.0
+    dma("Y", nm_in, tl("nm", 0, 128))
+    dma("Y", tl("xw", ROT, 2048), tl("xt", 0, 2048 - ROT))
+    dma("Y", tl("xw", 0, ROT), tl("xt", 2048 - ROT, 2048))
+    dma("Y", th_in, tl("th", 0, 1))
+    dma("Y", wt_in, tl("wt", 0, 1))
+
+    pi_ = iota(new("ti", 1), [[0, 1]], 0, 1)
+    col = iota(new("ti", 144), [[1, 144]], 0, 0)
+    ki = ts(new("ti", 1), pi_, 15, AL.bitwise_and)
+    kf = cp(new("cf", 1), ki)
+    pf = cp(new("cf", 1), pi_)
+    g16 = tt(new("cf", 1), pf, kf, AL.subtract)
+    cache = {}
+
+    def kcol(mul, off):
+        if ("k", mul, off) not in cache:
+            cache[("k", mul, off)] = ts(new("cf", 1), kf, float(mul), AL.mult, float(off), AL.add)
+        return cache[("k", mul, off)]
+    col128 = sub(col, 0, 128)
+    ident = ts(new("cb", 128), col128, pf, AL.is_equal)
+    colg = ts(new("ti", 128), col128, 112, AL.bitwise_and)
+    blk = ts(new("cb", 128), colg, g16, AL.is_equal)
+    turn = [0]
+    zeros = fill(new("cb", 128), 0.0)
+
+    def scaled(base, s):
+        key = (base, s)
+        if key not in cache:
+            turn[0] += 1
+            if s == 1:
+                cache[key] = base
+            elif isinstance(s, tuple) or 1e-20 < abs(s) < 1e20:
+                s_ = s if isinstance(s, tuple) else float(s)
+                if base == ident and s in PAR["onG"]:
+                    cache[key] = select(new("cb", 128), zeros, [[-1, 128]], AL.not_equal, s_, 1)
+                elif turn[0] % PAR["turn"] == 0:
+                    cache[key] = act(new("cb", 128), base, AF.Identity, 0.0, s_)
+                else:
+                    cache[key] = ts(new("cb", 128), base, s_, AL.mult)
+            else:
+                cache[key] = ts(new("cb", 128), base, 2.0 ** 60, AL.mult, float(s / 2.0 ** 60), AL.mult)
+        return cache[key]
+
+    def I(s=1):
+        return scaled(ident, s)
+
+    def B(s=1):
+        return scaled(blk, s)
+
+    def IBm(a, b):
+        if ("m", a, b) not in cache:
+            cache[("m", a, b)] = select(new("cb", 128), B(b), [[-1, 128]], AL.not_equal, a + b, 1)
+        return cache[("m", a, b)]
+    BIG = 2.0 ** 120
+    EPS = 1.0 / 128
+    IB = IBm(1.0, -0.4)
+    ones = fill(new("cb", 3 * HW), 1.0)
+    one = sub(ones, 0, HW)
+    blk32 = act(new("cf", 128), blk, AF.Identity)
+    TINY = scaled(ident, act(new("cf", 1), kf, AF.Exp, -75.0, 0.0, None, 1300.0))
+    k0 = ts(new("cf", 1), kf, 0.0, AL.is_equal, -999.0, AL.mult)
+    pm1 = ts(new("cf", 1), pf, -1.0, AL.add, k0, AL.add)
+    shf = ts(new("cb", 128), col128, pm1, AL.is_equal, -1.0, AL.mult)
+    DM = scaled(select(new("cb", 128), shf, [[-1, 128]], AL.not_equal, 1.0, 1), BIG / 2)
+    k15 = ts(new("cf", 1), kf, 15.0, AL.is_equal, 1.5 * 2.0 ** 60, AL.mult)
+    D15 = ts(new("cb", 128), ident, k15, AL.mult, 2.0 ** 60, AL.mult)
+    BK = scaled(blk, kcol(EPS, 2 * EPS))
+    BK1 = scaled(blk, kcol(EPS, 2 * EPS + 1))
+    g15 = ts(new("cf", 1), g16, 15.0, AL.add)
+    SEL = ts(new("cb", 144), col, g15, AL.is_equal)
+    colk = ts(new("ti", 128), col128, 15, AL.bitwise_and)
+    QK = tt(new("cb", 128), blk, ts(new("cb", 128), colk, -1.0, AL.mult, -183.0, AL.add), AL.mult)
+    offd = ts(new("cb", 128), colk, kf, AL.not_equal)
+    DG1 = act(new("cb", HW), sub(offd, 0, HW), AF.Identity, 0.0, -8192.0)
+    DG2 = act(new("cb", 128), offd, AF.Identity, -7.0 * 2 ** 17, -2.0 ** 20)
+    keep = new("cb", 512)
+    fill(keep, 1.0)
+    fill(sub(keep, 0, 512, 16), 0.0)
+    fill(tl("xw", 2048, 2064), 0.0)
+    ones32 = fill(new("cf", 128), 1.0)
+    TS = 2.0 ** 97 if "cf" in PAR["onS"].split() else 1.0
+    thp = ts(new("cf", 1), th_in, 53248.5, AL.add, TS, AL.mult)
+    keep3 = new("cb", 3 * HW)
+    fill(keep3, 1.0)
+    fill(sub(keep3, 0, 3 * HW, 3), 0.0)
+    key32 = act(new("cf", 128), ident, AF.Identity, 0.0, 2.0 ** 19)
+    BW = scaled(blk, cp(new("cf", 1), wt_in))
+    bi = ts(new("ti", 8), iota(new("ti", 8), [[16, 8]], ROT // 16, 0), kf, AL.add)
+    bases = ts(new("cf", 8), ts(new("ti", 8), bi, 127, AL.bitwise_and), 16.0, AL.mult)
+
+    def slot(t, x):
+        lb = tl("lb", (2 * t + x) * LB, (2 * t + x + 1) * LB)
+        lf = tl("lf", (2 * t + x) * LF, (2 * t + x + 1) * LF)
+        return {"lb": lb, "lf": lf, "H": sub(lb, 0, HW), "E": sub(lb, HW, 4 * HW), "HE": sub(lb, 0, 4 * HW),
+                "Q": sub(lb, 4 * HW, 5 * HW), "N": sub(lf, 0, HW), "cnt": sub(lf, HW + t % 2, HW + t % 2 + 1),
+                "old": sub(lf, HW + 1 - t % 2, HW + 2 - t % 2), "padf": sub(lf, HW, LF)}
+
+    def pl(t, d):
+        return sub(t, d * HW, (d + 1) * HW)
+
+    def il(t, d):
+        return sub(t, d, 3 * HW, 3)
+    tmp = {}
+    both = {"xc": new("tb", 2 * HW), "ys": new("tb", 32 * HW), "KPs": new("tb", 2 * HW), "O": new("tb", 2 * HW)}
+
+    def tmpf(x):
+        def get(name, buf="tb", n=HW, parts=128):
+            if name in both:
+                w_ = nel(both[name]) // 2
+                return sub(both[name], x * w_, (x + 1) * w_)
+            if (x, name) not in tmp:
+                tmp[(x, name)] = new(buf, n, parts)
+            return tmp[(x, name)]
+        return get
+
+    def bank(x, which, a, n=1, parts=128):
+        b = {"u": x, "a": 4 + 2 * x, "b": 5 + 2 * x}[which]
+        return tl("pb%d" % b, a * HW, (a + n) * HW, 1, parts)
+
+    def encode(x):
+        s, m = slot(0, x), tmpf(x)
+        c0 = x * HW
+        ps, dv, ex = sub(ps_in, c0, c0 + HW), sub(dv_in, c0, c0 + HW), sub(ex_in, 3 * c0, 3 * c0 + 3 * HW)
+        tt(s["Q"], ts(m("r"), ps, kcol(-1, 9), AL.add), ts(m("Pd"), ps, 0.0, AL.is_lt, kcol(1, -16), AL.mult), AL.add)
+        vp = tt(m("u"), dv, ts(m("Fs"), ps, 0.0, AL.is_lt, 4.0, AL.mult), AL.add)
+        hm, e0 = m("tP", n=3 * HW), m("st", n=3 * HW)
+        cd = act(sub(m("eq", n=4 * HW), 0, 3 * HW), ex, AF.Identity, 2 * EPS, EPS)
+        op = ts(m("gg", n=3 * HW), ex, -1.0, AL.is_equal)
+        for d in range(3):
+            ts(pl(hm, d), vp, float(d), AL.is_equal)
+            tt(pl(e0, d), sub(cd, d, 3 * HW, 3), sub(op, d, 3 * HW, 3), AL.max)
+        nh = act(cd, hm, AF.Identity, 9.0, -10.0)
+        tt(s["E"], e0, nh, AL.min)
+        pr = tt(op, hm, e0, AL.mult)
+        ph = bank(x, "b", 0)
+        mm([(ph, I(), pl(pr, d)) for d in range(3)])
+        act(s["H"], ph, AF.Identity)
+        tt(s["N"], sub(nm_in, c0, c0 + HW), act(m("cP", "tf"), dv, AF.Identity, 8224.0, -4096.0), AL.add)
+        fill(s["padf"], 0.0)
+        dk = m("dnk", "tf", 3 * HW)
+        for d in range(3):
+            ts(il(dk, d), sub(dn_in, 3 * c0 + d, 3 * c0 + 3 * HW, 3), float(32 + 4096 * (2 - d) + 2 ** 18), AL.add, 2.0 ** -19, AL.mult)
+
+    XG, XW = tl("xw", 0, 2064), tl("xw", 0, 4112)
+    AQ = 0.61
+    thrs = {0: thp}
+    onS = PAR["onS"].split()
+
+    def visit(t, x):
+        s, m = slot(t, x), tmpf(x)
+        Q, N, E, HE = s["Q"], s["N"], s["E"], s["HE"]
+        dk = m("dnk", "tf", 3 * HW)
+        r = act(m("r"), Q, AF.Exp, kcol(-AQ, AQ * (9 + 106)), -AQ)
+        p1 = bank(x, "a", 0)
+        mm([(p1, IB, r)])
+        fp = act(m("Fp"), Q, AF.Relu, kcol(1, -8))
+        fs = act(m("Fs"), Q, AF.Sign, 7.5)
+        if "P" in onS:
+            P, pa, pb = act(m("P"), p1, AF.Sign), 3.0, 3.0
+        else:
+            P, pa, pb = ts(m("P"), p1, 0.0, AL.is_gt), 6.0, 0.0
+        px = bank(x, "b", 2)
+        mm([(px, I(), pl(E, d)) for d in range(3)] + [(px, I(4), fp)])
+        pc = tt(m("Pc"), P, px, AL.is_gt)
+        u = act(m("u"), Q, AF.Exp, kcol(AQ, -AQ * (9 + 113.5)), AQ)
+        tP = m("tP", n=3 * HW)
+        for d in range(3):
+            tt(pl(tP, d), pl(E, d), pc, AL.mult)
+        pm = bank(x, "a", 1, 3)
+        mm([(pm, B(), tP)])
+        st = act(m("st", n=3 * HW), pm, AF.Sign, kcol(-EPS, -1.5 * EPS))
+        pcn = bank(x, "a", 4)
+        mm([(pcn, D15, one)] + [(pcn, DM, pl(st, d)) for d in range(3)])
+        tw = tt(m("t"), u, pcn, AL.min)
+        p2, p2j = bank(x, "a", 5), bank(x, "b", 7)
+        mm([(p2, TINY, P), (p2, IB, tw)])
+        mm([(p2j, IB, tw)])
+        zn = act(m("Zn"), px, AF.Relu, 1.0, -64.0)
+        pz = bank(x, "b", 0)
+        mm([(pz, B(), fs)])
+        zf = act(m("Zf"), pz, AF.Relu, -15.0)
+        pw = bank(x, "b", 3, 3)
+        mm([(il(pw, d), I(), pl(E, d)) for d in range(3)] + [(il(pw, 0), I(4), zn), (il(pw, 0), I(4), zf)])
+        w = tt(m("w", "tf", 3 * HW), dk, pw, AL.min)
+        gg = act(m("gg", n=3 * HW), pw, AF.Sign, -0.5)
+        cl = il(scan(m("cl", "tf", 3 * HW), keep3, w), 2)
+        cc = ts(m("cc", "ti"), ts(m("ci", "ti"), cl, 2.0 ** 19, AL.mult), 4095, AL.bitwise_and)
+        nn = ts(m("nn", "ti"), ts(m("ni", "ti"), N, float(ROT - 32), AL.add), 4095, AL.bitwise_and)
+        Pp = ts(m("Pp"), p2, 0.0, AL.is_gt)
+        js = act(m("Js"), p2j, AF.Sign, -2.0 ** -110, 1.0, s["cnt"] if t < NV - 1 else None)
+        cP = tt(m("cP", "tf"), cc, Pp, AL.mult)
+        pcv = bank(x, "a", 7)
+        mm([(pcv, blk32, cP)])
+        pum = bank(x, "a", 4)
+        mm([(pum, I(-1024), fs), (pum, IBm(2048.0, 1024.0), Pp)])
+        pct = bank(x, "a", 1)
+        mm([(pct, I(), DG1), (pct, blk32, cP)])
+        pr = tt(m("pr", "ti"), nn, pcv, AL.mult)
+        xi = ts(m("xi", "ti"), pr, 5, AL.arith_shift_right, 2047, AL.bitwise_and)
+        off = ts(m("off", "tu"), tt(m("xo", "tf"), xi, pum, AL.max), 2048.0, AL.min)
+        sc = scan(m("sc", "tf"), sub(keep, 0, HW), pct)
+        c1 = ts(m("c1", "ti", 4), sub(sc, 15, HW, 16), float(ROT - 32), AL.add)
+        c3 = cp(m("c3", "tu", 4), ts(m("c2", "ti", 4), c1, 2047, AL.bitwise_and))
+        xc = gather("S", m("xc"), XG, c3)
+        y, ad = m("y", n=16 * HW), m("ad", n=16 * HW)
+        for (e_, a, b) in PAR["gather"]:
+            gather(e_, sub(y, 16 * a, 16 * b), XG, sub(off, a, b))
+        for c in range(2):
+            pdd = tl("pb%d" % (2 + c), 0, 512)
+            mm([(pl(pdd, k), ident, xc) for k in range(8)], True, False)
+            mm([(pl(pdd, k), I(-1), sub(y, 8 * c + k, 16 * HW, 16)) for k in range(8)], False, True)
+            act(sub(ad, 512 * c, 512 * c + 512), pdd, AF.Abs)
+        kps = act(m("KPs"), cP, AF.Sign, -16.0)
+        pD = bank(x, "a", 0)
+        lanes = [(pD, sub(SEL, 15 - k, 143 - k), pl(ad, k)) for k in range(16)]
+        mm([(pD, I(-4096), fs), (pD, I(8192), Pp), (pD, B(-4096), kps)] + lanes[:8], True, False)
+        mm(lanes[8:], False, True)
+        pq = bank(x, "b", 1)
+        pd = act(m("Pd"), Q, AF.Relu, -8.0, -1.0)
+        qn = ts(m("Qn"), Q, -8.0, AL.max)
+        mm([(pq, I(-1), pd), (pq, I(-8), js), (pq, IBm(-512.0, 496.0), Pp)])
+        tt(Q, qn, pq, AL.min)
+        pt2 = bank(x, "b", 6)
+        mm([(pt2, I(), tw), (pt2, I(-BIG), Pp)])
+        t2 = act(m("t2"), pt2, AF.Relu)
+        p3 = bank(x, "b", 7)
+        mm([(p3, IB, t2)])
+        if "J2" in onS:
+            j2, jm, jb = act(m("J2"), p3, AF.Sign, -2.0 ** -110), scaled(BK, 0.5), 0.59375
+        else:
+            j2, jm, jb = ts(m("J2"), p3, 0.0, AL.is_gt), BK, 0.0
+        pR = bank(x, "b", 2, 4)
+        mm([(pl(pR, d), BK, Pp) for d in range(4)])
+        eq = tt(m("eq", n=4 * HW), HE, pR, AL.is_equal)
+        pcm = bank(x, "b", 6)
+        mm([(pcm, I(pa), P), (pcm, I(6), zn), (pcm, I(6), zf), (pcm, I(4), js), (pcm, jm, j2)])
+        cm = act(m("cm"), pcm, AF.Identity, -6.0 + pb + jb)
+        prs = bank(x, "b", 2, 4)
+        pe3 = sub(prs, HW, 4 * HW)
+        mm([(pl(prs, 0), I(), pl(eq, 0)), (pl(prs, 0), I(), Pp), (pe3, I(12), sub(eq, HW, 4 * HW)), (pe3, I(-2), E)]
+           + [(pl(pe3, d), I(), cm) for d in range(3)])
+        tt(HE, HE, prs, AL.max)
+        pup = bank(x, "b", 1)
+        mm([(pup, I(), u), (pup, I(-BIG), Pp)])
+        up = act(m("up"), pup, AF.Relu)
+        pY = bank(x, "b", 7)
+        mm([(pY, IB, up)])
+        if "nq" in onS:
+            pn = bank(x, "b", 1)
+            mm([(pn, I(), fp), (pn, I(256), act(m("Yh"), pY, AF.Sign))])
+            nq = act(m("nq"), pn, AF.Relu, -256.0)
+        else:
+            nq = tt(m("nq"), ts(m("Yh"), pY, 0.0, AL.is_gt), fp, AL.mult)
+        U = bank(x, "u", 0, 5)
+        ub = [pl(U, i) for i in range(5)]
+        mm([(ub[d], I(-8), il(gg, d)) for d in range(3)]
+           + [(ub[1], I(8), il(gg, 0)), (ub[2], I(8), il(gg, 0)), (ub[2], I(8), il(gg, 1))], True, False)
+        mm([(ub[4], key32, cl)], False, False)
+        mm([(ub[0], IBm(-16.0, 23.0), Pp), (ub[1], IBm(-16.0, 31.0), Pp), (ub[2], IBm(-16.0, 39.0), Pp), (ub[3], QK, Pp),
+            (ub[4], I(16384 * (t - 31)), Pp)], False, False)
+        mm([(ub[3], I(192), kps), (ub[4], I(2 ** 19), kps)], False, False)
+        mm([(ub[3], B(), nq)], False, False)
+        if t not in thrs:
+            mt = tmpf(2)
+            pt = sub(bank(x, "b", 7), 0, 1)
+            mm([(pt, ones32, slot(t, 0)["old"]), (pt, ones32, slot(t, 1)["old"])])
+            a7 = ts(mt("a7", "ti", 1), ts(mt("tot", "ti", 1), pt, 0.5, AL.mult), 7, AL.bitwise_and)
+            thrs[t] = ts(mt("thr%d" % t, "tf", 1), a7, 32.0 * TS, AL.mult, thp, AL.add)
+        if "cf" in onS:
+            tO = tt(m("tO"), act(m("cf"), pD, AF.Relu, thrs[t], -TS), r, AL.min)
+        else:
+            tO = tt(m("tO"), ts(m("cf"), pD, thrs[t], AL.is_le), r, AL.mult)
+        p4 = bank(x, "a", 4)
+        mm([(p4, IB, tO)])
+        O = ts(m("O"), p4, 0.0, AL.is_gt)
+        mm([(ub[0], BK1, O), (ub[1], BK1, O), (ub[2], BK1, O), (ub[3], B(-384), O), (ub[4], B(-2 ** 20), O)], False, True)
+        tt(E, E, sub(U, 0, 3 * HW), AL.min)
+        tt(Q, Q, ub[3], AL.max)
+        tt(N, N, ub[4], AL.max)
+        if t < NV - 1:
+            n = slot(t + 1, x)
+            for j, z in enumerate(["lb", "lf"]):
+                i = add("G", "send", (s[z], n[z], 4 * t + 2 * x + j), [s[z]], [], PAR["issue"])
+                add(None, "recv", (4 * t + 2 * x + j,), [], [n[z]], PAR["flight"], [i])
+        for c in range(2):
+            scan(sub(m("ys"), 512 * c, 512 * c + 512), keep, sub(y, 512 * c, 512 * c + 512))
+
+    def table():
+        m = tmpf(2)
+        Y = sub(both["ys"], 15, 32 * HW, 16)
+        pv = tl("pb2", 0, 128)
+        mm([(pv, I(0.5), both["xc"]), (pv, I(0.5), Y)])
+        vi = ts(m("vi", "ti", 128), pv, -0.25, AL.add)
+        ph = tl("pb3", 0, 128)
+        mm([(ph, I(), DG2), (ph, BW, Y), (ph, B(-65536), both["KPs"]), (ph, B(131072), both["O"])])
+        sc = scan(m("sc", "tf", 128), sub(keep, 0, 128), ph)
+        h1 = cp(m("h1", "ti", 8), sub(sc, 15, 128, 16))
+        h2 = ts(m("h2", "ti", 8), h1, 131072 + 15, AL.bitwise_and)
+        h3 = ts(m("h3", "tf", 8), h2, 2064.0, AL.min)
+        h5 = cp(m("h5", "tu", 8), tt(m("h4", "tf", 8), h3, bases, AL.add))
+        add("V", "sca", (XW, h5, vi), [h5, vi], [XW], 128 * PAR["sca"] * PAR["cyc"] + 50.0)
+
+    def decode(x):
+        s, m = slot(NV - 1, x), tmpf(x)
+        c0 = x * HW
+        ni = cp(m("ni", "ti"), s["N"])
+        ts(tl("of", c0, c0 + HW), ts(m("nn", "ti"), ni, 4095, AL.bitwise_and), -32.0, AL.add)
+        ts(tl("ob", 128 + c0, 128 + c0 + HW), ts(m("cc", "ti"), ni, 12, AL.arith_shift_right, 3, AL.bitwise_and), -1.0, AL.mult, 2.0, AL.add)
+        tt(tl("ob", c0, c0 + HW), ts(m("r"), s["Q"], kcol(1, -9), AL.add, -1.0, AL.max), ts(m("u"), s["Q"], -8.0, AL.is_lt), AL.subtract)
+        pw = bank(x, "a", 1, 3)
+        mm([(pw, I(-4), sub(ones, 0, 3 * HW)), (pw, I(-4), s["E"])] + [(pl(pw, d), I(), s["H"]) for d in range(3)])
+        e1 = tt(m("tP", n=3 * HW), s["E"], pw, AL.max)
+        xx = ts(m("st", n=3 * HW), e1, 1.0, AL.min, 128.0, AL.mult)
+        sg = act(m("gg", n=3 * HW), e1, AF.Sign, -0.5)
+        po = bank(x, "a", 5, 3)
+        mm([(po, I(), xx), (po, I(-63.5), sg)])
+        for d in range(3):
+            act(tl("ob", 256 + 3 * c0 + d, 256 + 3 * c0 + 3 * HW, 3), pl(po, d), AF.Identity, -65.5)
+
+    for x in range(2):
+        lead[0], lead[1] = PAR["lead0"] * (1 - x), 0
+        encode(x)
+    for t in range(NV):
+        lead[1] = 0 if t == 0 else (2 if t == NV - 1 else 1)
+        for x in range(2):
+            lead[0] = PAR["lead" if t else "lead0"] * (1 - x)
+            visit(t, x)
+        table()
+    decode(0)
+    decode(1)
+    dma("Y", tl("yx", 0, 2048 - ROT), tl("xw", ROT, 2048))
+    dma("S", tl("yx", 2048 - ROT, 2048), tl("xw", 0, ROT))
+    dma("Y", tl("yn", 0, 128), tl("of", 0, 128))
+    dma("Y", tl("yp", 0, 128), tl("ob", 0, 128))
+    dma("Y", tl("yd", 0, 128), tl("ob", 128, 256))
+    dma("Y", tl("yg", 0, 384), tl("ob", 256, 640))
+    return ops
+
+
+def schedule(ops, shift):
+    n = len(ops)
+    lat = [o["cost"] + (PAR["dma"] if o["kind"] == "dma" else 0.0) for o in ops]
+    succ = [[] for _ in ops]
+    for i, o in enumerate(ops):
+        for j in o["deps"]:
+            succ[j].append(i)
+    prio = [0.0] * n
+    for i in range(n - 1, -1, -1):
+        prio[i] = lat[i] + max([prio[j] + PAR["cross"] for j in succ[i]] + [0.0])
+    rank_ = [prio[i] + o["lead"] + shift.get(o["role"], 0.0) for i, o in enumerate(ops)]
+    for i in range(n - 1, -1, -1):
+        if ops[i]["const"] and succ[i]:
+            rank_[i] = lat[i] + PAR["cross"] + max(rank_[j] for j in succ[i]) + shift.get(ops[i]["role"], 0.0)
+    left = [len(o["deps"]) for o in ops]
+    ready = [i for i in range(n) if not left[i]]
+    fin = [0.0] * n
+    base = [0.0] * n
+    free = {}
+    lastb = {}
+    held = {}
+    order = []
+    while ready:
+        cand = []
+        for i in ready:
+            o = ops[i]
+            if o["kind"] == "mm" and o["args"][1] and any(held.get(b) for b in o["banks"]):
+                continue
+            st = max(base[i], free.get(o["eng"], 0.0) if o["eng"] else 0.0)
+            for b in o["banks"]:
+                for e, j in lastb.get(b, {}).items():
+                    if e != o["eng"]:
+                        st = max(st, fin[j] + PAR["cross"])
+            cand.append((st, i))
+        t0, i0 = min(cand, key=lambda c: c[0] + PAR["look"] * ops[c[1]]["cost"])
+        t0 += PAR["look"] * ops[i0]["cost"]
+        st, i = max([c for c in cand if c[0] <= t0 and ops[c[1]]["eng"] == ops[i0]["eng"]],
+                    key=lambda c: rank_[c[1]])
+        o = ops[i]
+        o["waits"] = set(o["deps"])
+        for b in o["banks"]:
+            for e, j in lastb.get(b, {}).items():
+                if e != o["eng"]:
+                    o["waits"].add(j)
+            lastb.setdefault(b, {})[o["eng"]] = i
+            if o["kind"] == "mm":
+                held[b] = not o["args"][2]
+        fin[i] = st + lat[i]
+        if o["eng"]:
+            free[o["eng"]] = st + o["cost"]
+        o["start"], o["prio"] = st, prio[i]
+        order.append(i)
+        ready.remove(i)
+        for j in succ[i]:
+            d = 0.0 if (o["eng"] == "P" and ops[j]["eng"] == "P") else (PAR["same"] if ops[j]["eng"] == o["eng"] else PAR["cross"])
+            base[j] = max(base[j], fin[i] + d)
+            left[j] -= 1
+            if not left[j]:
+                ready.append(j)
+    assert len(order) == n
+    return order, max(fin)
+
+
+def search(ops):
+    roles = sorted(set(o["role"] for o in ops))
+    seed = [PAR["seed"]]
+
+    def rnd():
+        seed[0] = (seed[0] * 1103515245 + 12345) % 2147483648
+        return seed[0] / 2147483648.0
+
+    def delays(order):
+        prev, last = {}, {}
+        fin = {i: ops[i]["start"] + ops[i]["cost"] + (PAR["dma"] if ops[i]["kind"] == "dma" else 0.0) for i in order}
+        for i in order:
+            if ops[i]["eng"]:
+                prev[i] = last.get(ops[i]["eng"])
+                last[ops[i]["eng"]] = i
+        i = max(order, key=lambda j: fin[j])
+        out = []
+        while True:
+            c = [(fin[j], j) for j in ops[i]["waits"]]
+            if prev.get(i) is not None:
+                c.append((ops[prev[i]]["start"] + ops[prev[i]]["cost"] - 60.0, prev[i]))
+            if not c:
+                return out
+            j = max(c)[1]
+            if j not in ops[i]["deps"]:
+                out.append((i, j))
+            i = j
+    shift = {}
+    order, cur = schedule(ops, shift)
+    best, kept, q = cur, {}, delays(order)
+    for it in range(PAR["iters"]):
+        tr = dict(shift)
+        for _k in range(1 + int(rnd() * 2.5)):
+            if rnd() < 0.7 and q:
+                i, j = q[int(rnd() * len(q))]
+                r, sg = (ops[i]["role"], 1.0) if rnd() < 0.5 else (ops[j]["role"], -1.0)
+                tr[r] = tr.get(r, 0.0) + sg * rnd() * PAR["step"]
+            else:
+                r = roles[int(rnd() * len(roles))]
+                tr[r] = tr.get(r, 0.0) + (rnd() - 0.5) * 2 * PAR["step"]
+        order, v = schedule(ops, tr)
+        if v <= cur + 400.0 * (1.0 - it / PAR["iters"]) * rnd():
+            cur, shift, q = v, tr, delays(order)
+            if v < best:
+                best, kept = v, tr
+    return schedule(ops, kept)
+
+
+PLAN = {}
+
+
+def rank_program(g, core, T, topo):
+    rank = T.rank_of(core)
+    if rank is None:
+        return
+    if not PLAN:
+        PLAN["ops"] = build()
+        PLAN["order"] = search(PLAN["ops"])[0]
+    ops, order = PLAN["ops"], PLAN["order"]
+    nxt = T.cores[(rank + 1) % len(T.cores)]
+    rid, pid = topo.addr(nxt, core)
+    eng = topo.engines(core, nxt)
+    he = len(eng) // 2
+    queue = {"V": g.vector, "S": g.scalar, "P": g.tensor, "G": g, "Y": g.sync}
+    count = {}
+    token = {}
+    clock = {}
+    known = {k: {} for k in queue}
+    ndma = [0]
+
+    def ap(t):
+        if not isinstance(t, tuple):
+            return t
+        if t[0] not in SCRATCH and t[1] == 0 and t[2] == T[t[0]].shape[1]:
+            return T[t[0]][:]
+        if t[3] == 1:
+            return T[t[0]][0:t[4], t[1]:t[2]]
+        return T[t[0]][0:t[4], t[1]:t[2]:t[3]]
+
+    def win(w, off):
+        return T[w[0]][:, w[1]:w[2]].indirect(T[off[0]][:, off[1]:off[2]])
+
+    for i in order:
+        o = ops[i]
+        e, kind, a = o["eng"], o["kind"], o["args"]
+        if kind == "recv":
+            token[i] = ("arr%d" % a[0], 2 * he)
+            count[token[i][0]] = 2 * he
+            clock[i] = {token[i][0]: 2 * he}
+            continue
+        q, kn = queue[e], known[e]
+        need = {}
+        for j in o["waits"]:
+            if e == "P" and ops[j]["eng"] == "P":
+                continue
+            s_, v = token[j]
+            if v > need.get(s_, (0, 0))[0]:
+                need[s_] = (v, j)
+        for s_, (v, j) in sorted(need.items(), key=lambda z: -ops[z[1][1]]["start"]):
+            if kn.get(s_, 0) < v:
+                q.wait_ge(T.sem[s_], v)
+                for k_, v_ in clock[j].items():
+                    kn[k_] = max(kn.get(k_, 0), v_)
+        if kind == "send":
+            g.remote_dma(ap(a[1]), ap(a[0]), T.sem["arr%d" % a[2]], T.sem.sent, pid, rid, topo.mask(core, nxt))
+            count["sent"] = count.get("sent", 0) + 2 * he
+            continue
+        if kind == "ts":
+            if a[5] is None:
+                ins = q.tensor_scalar(ap(a[0]), ap(a[1]), ap(a[2]), None, a[4])
+            else:
+                ins = q.tensor_scalar(ap(a[0]), ap(a[1]), ap(a[2]), ap(a[3]), a[4], a[5])
+        elif kind == "tt":
+            ins = q.tensor_tensor(ap(a[0]), ap(a[1]), ap(a[2]), a[3])
+        elif kind == "cp":
+            ins = q.tensor_copy(ap(a[0]), ap(a[1]))
+        elif kind == "fill":
+            ins = q.memset(ap(a[0]), a[1])
+        elif kind == "scan":
+            ins = q.tensor_tensor_scan(ap(a[0]), ap(a[1]), ap(a[2]), 0.0, AL.mult, AL.max)
+        elif kind == "act":
+            ins = q.activation(ap(a[0]), ap(a[1]), a[2], bias=ap(a[3]), scale=ap(a[4]), accum_out=ap(a[5]))
+        elif kind == "gat":
+            if e == "S":
+                ins = q.activation(ap(a[0]), win(a[1], a[2]), AF.Identity)
+            else:
+                ins = q.tensor_copy(ap(a[0]), win(a[1], a[2]))
+        elif kind == "sca":
+            ins = q.tensor_copy(win(a[0], a[1]), ap(a[2]))
+        elif kind == "mm":
+            for k_, (o_, l_, r_) in enumerate(a[0]):
+                ins = q.matmul(ap(o_), ap(l_), ap(r_), a[1] and k_ == 0, a[2] and k_ == len(a[0]) - 1)
+        elif kind == "iota":
+            ins = g.iota(ap(a[0]), a[1], a[2], a[3])
+        elif kind == "sel":
+            ins = g.affine_select(ap(a[0]), ap(a[1]), a[2], a[3], a[4], 0, a[5])
+        elif kind == "dma":
+            ins = q.dma_start(ap(a[0]), ap(a[1]))
+        if kind == "dma":
+            s_, inc = "dma%d" % ndma[0], 16
+            ndma[0] += 1
+        else:
+            s_, inc = "q" + e, 1
+        ins.then_inc(T.sem[s_], inc)
+        count[s_] = count.get(s_, 0) + inc
+        token[i] = (s_, count[s_])
+        clock[i] = dict(kn)
+        clock[i][s_] = count[s_]
+    for s_, v in count.items():
+        g.wait_ge(T.sem[s_], v)

@@ -1,19 +1,26 @@
+from concourse.bass import DstId, RemoteDMATransfer
 from concourse.mybir import AluOpType, ActivationFunctionType
 
-HW = 64
+HW = 128
 NV = 6
 ROT = 1184
-LB, LF = 320, 68
+XC = 4112
+ST = 528
 SCRATCH = {
     "cb": ("sbuf", [128, 12288], "bfloat16"),
+    "ch": ("sbuf", [128, 512], "float16"),
     "cf": ("sbuf", [128, 1024], "float32"),
-    "tb": ("sbuf", [128, 12288], "bfloat16"),
+    "tb": ("sbuf", [128, 16384], "bfloat16"),
+    "th16": ("sbuf", [128, 1024], "float16"),
     "tf": ("sbuf", [128, 2048], "float32"),
-    "ti": ("sbuf", [128, 2048], "int32"),
+    "ti": ("sbuf", [128, 3072], "int32"),
     "tu": ("sbuf", [128, 256], "uint16"),
-    "xw": ("sbuf", [128, 4112], "bfloat16"),
-    "lb": ("sbuf", [128, 2 * NV * LB], "bfloat16"),
-    "lf": ("sbuf", [128, 2 * NV * LF], "float32"),
+    "xw": ("sbuf", [128, 5 * XC], "bfloat16"),
+    "lb": ("sbuf", [128, 2 * 768], "bfloat16"),
+    "li": ("sbuf", [128, 2 * 144], "int32"),
+    "ls": ("sbuf", [128, 4 * ST], "float16"),
+    "mo": ("sbuf", [128, NV * 144], "uint16"),
+    "mi": ("sbuf", [128, NV * 144], "uint16"),
     "inb": ("sbuf", [128, 640], "bfloat16"),
     "ini": ("sbuf", [128, 528], "int32"),
     "ob": ("sbuf", [128, 640], "bfloat16"),
@@ -22,15 +29,26 @@ SCRATCH = {
 for _b in range(8):
     SCRATCH["pb%d" % _b] = ("psum", [128, 512], "float32")
 NDMA = 16
-SEMAPHORES = ["qV", "qS", "qP", "qG", "sent"] + ["arr%d" % i for i in range(4 * (NV - 1))] + ["dma%d" % i for i in range(NDMA)]
+NARR = 13
+SEMAPHORES = ["qV", "qS", "qP", "qG", "sent"] + ["arr%d" % i for i in range(NARR)] + ["dma%d" % i for i in range(NDMA)]
 
 AL, AF = AluOpType, ActivationFunctionType
-WIDE = {"float32": 4, "int32": 4, "bfloat16": 2, "uint16": 2}
+WIDE = {"float32": 4, "int32": 4, "bfloat16": 2, "uint16": 2, "float16": 2}
 PAR = {"cyc": 1.0, "pe": 0.5, "vfix": 30.0, "sfix": 65.0, "same": 60.0, "cross": 100.0, "gat": 1.56, "sca": 3.5,
-       "issue": 1000.0, "flight": 2700.0, "dma": 2200.0, "look": 0.3, "lead": 3000.0, "lead0": 4000.0, "seed": 1, "iters": 1000, "step": 2000.0,
-       "gather": [("S", 0, 18), ("V", 18, 32), ("S", 32, 50), ("V", 50, 64)],
-       "onS": "J2 nq", "turn": 2,
-       "onG": [0.5, -63.5, -4, 192, 2 ** 19, 12, -2, 6, 256, 8, -8, -4096, 8192, -1024] + [16384 * (t - 31) for t in range(NV)]}
+       "issue": 1000.0, "flight": 2000.0, "rate": 80.0, "after": ["seth", "setq"], "dma": 2200.0, "seed": 1, "iters": 1500, "step": 3000.0,
+       "slack": 300.0, "share": 0.03,
+       "gather": [("S", 0, 24), ("V", 24, 72), ("S", 72, 104), ("V", 104, 136)],
+       "onS": "P J2 nq", "turn": 2, "ring": 3,
+       "onG": [0.5, 16, 256, 8, -8, 2048, 7328, -384, -63.5] + [32768 * (t + 1) for t in range(NV)]}
+AT = {"p1": (4, 0), "px": (5, 0), "pz": (5, 1), "pA": (6, 0), "pm": (7, 0), "pcn": (4, 1), "p2": (5, 2), "p2j": (6, 3),
+      "pcc": (7, 3), "pcv": (4, 2), "pct": (5, 3), "pD": (4, 0), "pq": (5, 0), "pt2": (6, 0), "p3": (7, 0), "pR": (5, 0),
+      "pcm": (6, 1), "prs": (7, 0), "pup": (6, 2), "pY": (6, 3), "pn": (5, 0), "pt": (6, 0), "U": (3, 0), "pN": (5, 1),
+      "p4": (4, 1), "pv": (6, 0), "ph": (7, 0), "enc": (6, 0), "pw": (6, 0), "po": (7, 0),
+      "pe": (5, 0), "pM": (6, 0), "pH": (5, 1)}
+AT.update({"pA": (0, 0), "p2j": (2, 3), "pm": (1, 0), "p2": (1, 3), "px": (2, 0), "pz": (2, 1), "pcn": (2, 2), "p1": (6, 3),
+           "U": (3, 0), "pD": (4, 0), "pcc": (4, 1), "pcv": (4, 2), "pct": (6, 2), "pR": (6, 0), "UQ": (5, 0), "pt2": (5, 1),
+           "p3": (5, 2), "pcm": (6, 3), "pup": (5, 1), "pY": (5, 2), "pn": (5, 3), "prs": (7, 0), "pN": (6, 0), "p4": (0, 0),
+           "pv": (1, 0), "ph": (2, 0)})
 
 
 def tl(buf, a, b, step=1, parts=128):
@@ -57,7 +75,8 @@ def build():
     ops = []
     top = {}
     acc = {}
-    lead = [0.0, -1]
+    names = {}
+    phase = [-1]
 
     def new(buf, n, parts=128):
         a = top.get(buf, 0)
@@ -65,7 +84,7 @@ def build():
         assert top[buf] <= SCRATCH[buf][1][1], buf
         return tl(buf, a, a + n, 1, parts)
 
-    def add(eng, kind, args, reads, writes, cost, extra=()):
+    def add(eng, kind, args, reads, writes, cost, extra=(), tag=None):
         i = len(ops)
         deps = set(extra)
         for t in reads:
@@ -85,8 +104,10 @@ def build():
         deps.discard(i)
         banks = set(t[0] for t in list(reads) + list(writes) if psum(t))
         w0 = (list(writes) + list(reads))[0]
-        role = (kind, w0[0], w0[1] % {"lb": 2 * LB, "lf": 2 * LF}.get(w0[0], 1 << 20), len(reads), lead[0] > 0, lead[1])
-        ops.append({"role": role, "const": w0[0] in ("cb", "cf") or lead[1] < 0, "eng": eng, "kind": kind, "args": args, "deps": deps, "cost": cost, "banks": banks, "lead": lead[0]})
+        name = tag or names.get((w0[0], w0[1]), "%s%d" % (w0[0], w0[1] % {"lb": 768, "li": 144, "xw": XC, "mo": 144, "mi": 144}.get(w0[0], 1 << 20)))
+        role = (kind, name, len(reads), phase[0])
+        ops.append({"role": role, "name": name, "const": w0[0] in ("cb", "cf", "ch") or phase[0] < 0, "eng": eng, "kind": kind,
+                    "args": args, "deps": deps, "cost": cost, "banks": banks})
         return i
 
     def vcost(n):
@@ -136,8 +157,22 @@ def build():
         add(eng, "gat", (out, win, off), [win, off], [out], nel(out) * PAR["gat"] * PAR["cyc"] + 60.0)
         return out
 
+    def scatter(win, msg):
+        add("V", "sca", (win, sub(msg, HW, HW + 8), sub(msg, 0, HW)), [msg], [win], HW * PAR["sca"] * PAR["cyc"] + 50.0)
+
     def dma(eng, out, a):
         add(eng, "dma", (out, a), [a] if a[0] in SCRATCH else [], [out] if out[0] in SCRATCH else [], 100.0)
+
+    narr = [0]
+    sends = []
+
+    def send(src, dst, hop, tag):
+        if not isinstance(dst, list):
+            dst, hop = [dst], [hop]
+        i = add("G", "send", (src, dst, narr[0], hop), [src], [], PAR["issue"], sends[-1:] if tag in PAR["after"] else (), tag=tag)
+        add(None, "recv", (narr[0], i), [], dst, PAR["flight"] + len(dst) * nel(src) * width(src) * 128 / PAR["rate"], [i], tag=tag)
+        sends.append(i)
+        narr[0] += 1
 
     def iota(out, pat, base, cm):
         add("G", "iota", (out, pat, base, cm), [], [out], 130.0 + 2.0 * nel(out))
@@ -147,14 +182,16 @@ def build():
         add("G", "sel", (out, a, pat, op, float(v), cm), [a], [out], 170.0 + 2.0 * nel(out))
         return out
 
+    def table(t):
+        b = max(t - 1, 0) * XC
+        return {"x": tl("xw", b, b + 2048), "g": tl("xw", b, b + 2064), "w": tl("xw", b, b + XC), "z": tl("xw", b + 2048, b + 2064)}
+
     ps_in, dv_in, ex_in = tl("inb", 0, 128), tl("inb", 128, 256), tl("inb", 256, 640)
     nm_in, dn_in, wt_in, th_in = tl("ini", 0, 128), tl("ini", 128, 512), tl("ini", 512, 513), tl("ini", 520, 521)
-    lead[0] = 1e6
     dma("Y", ps_in, tl("ps", 0, 128))
     dma("S", ex_in, tl("ex", 0, 384))
     dma("Y", dv_in, tl("dv", 0, 128))
     dma("S", dn_in, tl("dn", 0, 384))
-    lead[0] = 0.0
     dma("Y", nm_in, tl("nm", 0, 128))
     dma("Y", tl("xw", ROT, 2048), tl("xt", 0, 2048 - ROT))
     dma("Y", tl("xw", 0, ROT), tl("xt", 2048 - ROT, 2048))
@@ -209,12 +246,13 @@ def build():
             cache[("m", a, b)] = select(new("cb", 128), B(b), [[-1, 128]], AL.not_equal, a + b, 1)
         return cache[("m", a, b)]
     BIG = 2.0 ** 120
+    LN2 = 0.6931471805599453
     EPS = 1.0 / 128
     IB = IBm(1.0, -0.4)
     ones = fill(new("cb", 3 * HW), 1.0)
     one = sub(ones, 0, HW)
-    blk32 = act(new("cf", 128), blk, AF.Identity)
-    TINY = scaled(ident, act(new("cf", 1), kf, AF.Exp, -75.0, 0.0, None, 1300.0))
+    B16, I16, H16 = cp(new("ch", 128), blk), cp(new("ch", 128), ident), ts(new("ch", 128), ident, 0.5, AL.mult)
+    TINY = ts(new("cb", 128), ident, 2.0 ** -54, AL.mult, 2.0 ** -54, AL.mult)
     k0 = ts(new("cf", 1), kf, 0.0, AL.is_equal, -999.0, AL.mult)
     pm1 = ts(new("cf", 1), pf, -1.0, AL.add, k0, AL.add)
     shf = ts(new("cb", 128), col128, pm1, AL.is_equal, -1.0, AL.mult)
@@ -226,271 +264,287 @@ def build():
     g15 = ts(new("cf", 1), g16, 15.0, AL.add)
     SEL = ts(new("cb", 144), col, g15, AL.is_equal)
     colk = ts(new("ti", 128), col128, 15, AL.bitwise_and)
-    QK = tt(new("cb", 128), blk, ts(new("cb", 128), colk, -1.0, AL.mult, -183.0, AL.add), AL.mult)
+    QK = tt(new("cb", 128), blk, ts(new("cb", 128), colk, 183.0, AL.add), AL.mult)
     offd = ts(new("cb", 128), colk, kf, AL.not_equal)
-    DG1 = act(new("cb", HW), sub(offd, 0, HW), AF.Identity, 0.0, -8192.0)
-    DG2 = act(new("cb", 128), offd, AF.Identity, -7.0 * 2 ** 17, -2.0 ** 20)
+    DG1 = act(new("cb", 128), offd, AF.Identity, 0.0, -8192.0)
+    DG2 = new("cb", 144)
+    act(sub(DG2, 0, 128), offd, AF.Identity, -7.0 * 2 ** 17, -2.0 ** 23)
+    fill(sub(DG2, 128, 143), -2.0 ** 23)
+    fill(sub(DG2, 143, 144), 16384.0)
+    B2k = scaled(blk, act(new("cf", 1), kf, AF.Exp, 0.0, LN2, None, 1300.0))
+    first_exp = len(ops) - 2
     keep = new("cb", 512)
     fill(keep, 1.0)
     fill(sub(keep, 0, 512, 16), 0.0)
-    fill(tl("xw", 2048, 2064), 0.0)
+    for t in range(1, NV):
+        fill(table(t)["z"], 0.0)
     ones32 = fill(new("cf", 128), 1.0)
-    TS = 2.0 ** 97 if "cf" in PAR["onS"].split() else 1.0
-    thp = ts(new("cf", 1), th_in, 53248.5, AL.add, TS, AL.mult)
-    keep3 = new("cb", 3 * HW)
-    fill(keep3, 1.0)
-    fill(sub(keep3, 0, 3 * HW, 3), 0.0)
-    key32 = act(new("cf", 128), ident, AF.Identity, 0.0, 2.0 ** 19)
-    BW = scaled(blk, cp(new("cf", 1), wt_in))
     bi = ts(new("ti", 8), iota(new("ti", 8), [[16, 8]], ROT // 16, 0), kf, AL.add)
     bases = ts(new("cf", 8), ts(new("ti", 8), bi, 127, AL.bitwise_and), 16.0, AL.mult)
 
-    def slot(t, x):
-        lb = tl("lb", (2 * t + x) * LB, (2 * t + x + 1) * LB)
-        lf = tl("lf", (2 * t + x) * LF, (2 * t + x + 1) * LF)
-        return {"lb": lb, "lf": lf, "H": sub(lb, 0, HW), "E": sub(lb, HW, 4 * HW), "HE": sub(lb, 0, 4 * HW),
-                "Q": sub(lb, 4 * HW, 5 * HW), "N": sub(lf, 0, HW), "cnt": sub(lf, HW + t % 2, HW + t % 2 + 1),
-                "old": sub(lf, HW + 1 - t % 2, HW + 2 - t % 2), "padf": sub(lf, HW, LF)}
-
-    def pl(t, d):
-        return sub(t, d * HW, (d + 1) * HW)
-
-    def il(t, d):
-        return sub(t, d, 3 * HW, 3)
+    def pl(t, d, n=1):
+        return sub(t, d * HW, (d + n) * HW)
     tmp = {}
-    both = {"xc": new("tb", 2 * HW), "ys": new("tb", 32 * HW), "KPs": new("tb", 2 * HW), "O": new("tb", 2 * HW)}
 
-    def tmpf(x):
-        def get(name, buf="tb", n=HW, parts=128):
-            if name in both:
-                w_ = nel(both[name]) // 2
-                return sub(both[name], x * w_, (x + 1) * w_)
-            if (x, name) not in tmp:
-                tmp[(x, name)] = new(buf, n, parts)
-            return tmp[(x, name)]
-        return get
+    def m(name, buf="tb", n=HW):
+        if name not in tmp:
+            tmp[name] = new(buf, n)
+            names[(buf, tmp[name][1])] = name
+        return tmp[name]
 
-    def bank(x, which, a, n=1, parts=128):
-        b = {"u": x, "a": 4 + 2 * x, "b": 5 + 2 * x}[which]
-        return tl("pb%d" % b, a * HW, (a + n) * HW, 1, parts)
+    def at(name, n=1):
+        b, a = AT[name]
+        names[("pb%d" % b, a * HW)] = name
+        return tl("pb%d" % b, a * HW, (a + n) * HW)
 
-    def encode(x):
-        s, m = slot(0, x), tmpf(x)
-        c0 = x * HW
-        ps, dv, ex = sub(ps_in, c0, c0 + HW), sub(dv_in, c0, c0 + HW), sub(ex_in, 3 * c0, 3 * c0 + 3 * HW)
-        tt(s["Q"], ts(m("r"), ps, kcol(-1, 9), AL.add), ts(m("Pd"), ps, 0.0, AL.is_lt, kcol(1, -16), AL.mult), AL.add)
-        vp = tt(m("u"), dv, ts(m("Fs"), ps, 0.0, AL.is_lt, 4.0, AL.mult), AL.add)
+    def state(t):
+        j = min(t, 1)
+        lb, li = tl("lb", j * 768, (j + 1) * 768), tl("li", j * 144, (j + 1) * 144)
+        return {"EQ": pl(lb, 0, 4), "E": pl(lb, 0, 3), "Q": pl(lb, 3), "HP": pl(lb, 4, 2), "H": pl(lb, 4), "P0": pl(lb, 5),
+                "li": sub(li, 0, HW + 9), "N": sub(li, 0, HW), "h2": sub(li, HW, HW + 9), "a7": sub(li, HW + 8, HW + 9)}
+
+    def fixed(j):
+        z = tl("ls", j * ST, (j + 1) * ST)
+        return {"all": z, "dl": pl(z, 0, 3), "c0": pl(z, 3), "th": sub(z, 512, 513), "wt": sub(z, 513, 514), "pad": sub(z, 512, ST)}
+    made = {}
+
+    def derived(j):
+        if j not in made:
+            f = fixed(j)
+            made[j] = (ts(new("tf", 1), f["th"], 2040.0 + 917504.5, AL.add), ts(new("tb", 128), blk, cp(new("tf", 1), f["wt"]), AL.mult))
+        return made[j]
+
+    def encode():
+        s, f = state(0), fixed(0)
+        ps, dv, ex = ps_in, dv_in, ex_in
+        tt(s["Q"], ts(m("r"), ps, -1.0, AL.mult, kcol(1, -9), AL.add), ts(m("fp"), ps, 0.0, AL.is_lt, kcol(-1, 16), AL.mult), AL.add)
+        vp = tt(m("u"), dv, ts(m("fu"), ps, 0.0, AL.is_lt, 4.0, AL.mult), AL.add)
         hm, e0 = m("tP", n=3 * HW), m("st", n=3 * HW)
-        cd = act(sub(m("eq", n=4 * HW), 0, 3 * HW), ex, AF.Identity, 2 * EPS, EPS)
-        op = ts(m("gg", n=3 * HW), ex, -1.0, AL.is_equal)
+        cd = act(m("eq", n=3 * HW), ex, AF.Identity, 2 * EPS, EPS)
+        ops[-1]["deps"].add(first_exp)
+        op = ts(m("gg", n=3 * HW), ex, -1.0, AL.is_equal, 2.0, AL.mult)
         for d in range(3):
             ts(pl(hm, d), vp, float(d), AL.is_equal)
             tt(pl(e0, d), sub(cd, d, 3 * HW, 3), sub(op, d, 3 * HW, 3), AL.max)
         nh = act(cd, hm, AF.Identity, 9.0, -10.0)
         tt(s["E"], e0, nh, AL.min)
         pr = tt(op, hm, e0, AL.mult)
-        ph = bank(x, "b", 0)
+        ph = at("enc")
         mm([(ph, I(), pl(pr, d)) for d in range(3)])
         act(s["H"], ph, AF.Identity)
-        tt(s["N"], sub(nm_in, c0, c0 + HW), act(m("cP", "tf"), dv, AF.Identity, 8224.0, -4096.0), AL.add)
-        fill(s["padf"], 0.0)
-        dk = m("dnk", "tf", 3 * HW)
-        for d in range(3):
-            ts(il(dk, d), sub(dn_in, 3 * c0 + d, 3 * c0 + 3 * HW, 3), float(32 + 4096 * (2 - d) + 2 ** 18), AL.add, 2.0 ** -19, AL.mult)
+        tt(s["N"], nm_in, act(m("sc", "tf"), dv, AF.Identity, float(ROT + 8192), -4096.0), AL.add)
+        cs = [sub(dn_in, d, 3 * HW, 3) for d in range(3)]
+        tt(pl(f["dl"], 0), cs[0], cs[1], AL.subtract)
+        tt(pl(f["dl"], 1), cs[1], cs[2], AL.subtract)
+        ts(pl(f["dl"], 2), cs[2], -2048.0, AL.add)
+        ts(f["c0"], cs[0], -2048.0, AL.add)
+        fill(f["pad"], 0.0)
+        ts(f["th"], th_in, -2040.0, AL.add)
+        cp(f["wt"], wt_in)
+        send(f["all"], [fixed(j)["all"] for j in range(1, 4)], [-1, -2, -3], "fix")
 
-    XG, XW = tl("xw", 0, 2064), tl("xw", 0, 4112)
     AQ = 0.61
-    thrs = {0: thp}
     onS = PAR["onS"].split()
 
-    def visit(t, x):
-        s, m = slot(t, x), tmpf(x)
-        Q, N, E, HE = s["Q"], s["N"], s["E"], s["HE"]
-        dk = m("dnk", "tf", 3 * HW)
-        r = act(m("r"), Q, AF.Exp, kcol(-AQ, AQ * (9 + 106)), -AQ)
-        p1 = bank(x, "a", 0)
+    def visit(t):
+        s, X = state(t), table(t)
+        j = (t - 1) % 4 if t else 0
+        f = fixed(j)
+        thp, BW = derived(j)
+        Q, N, E, EQ = s["Q"], s["N"], s["E"], s["EQ"]
+        if 0 < t < NV - 1:
+            send(X["x"], table(t + 1)["x"], -1, "tab")
+        r = act(m("r"), Q, AF.Exp, kcol(-AQ, AQ * (9 + 106)), AQ)
+        p1 = at("p1")
         mm([(p1, IB, r)])
-        fp = act(m("Fp"), Q, AF.Relu, kcol(1, -8))
-        fs = act(m("Fs"), Q, AF.Sign, 7.5)
+        fp = act(m("fp"), Q, AF.Relu, kcol(4, -32), -4.0)
+        fu = act(m("fu"), Q, AF.Relu, -7.0)
         if "P" in onS:
-            P, pa, pb = act(m("P"), p1, AF.Sign), 3.0, 3.0
+            P = act(m("P"), p1, AF.Sign)
         else:
-            P, pa, pb = ts(m("P"), p1, 0.0, AL.is_gt), 6.0, 0.0
-        px = bank(x, "b", 2)
-        mm([(px, I(), pl(E, d)) for d in range(3)] + [(px, I(4), fp)])
-        pc = tt(m("Pc"), P, px, AL.is_gt)
-        u = act(m("u"), Q, AF.Exp, kcol(AQ, -AQ * (9 + 113.5)), AQ)
+            P = ts(m("P"), p1, 0.0, AL.is_gt, 0.5, AL.subtract)
+        px, pz = at("px", 2), at("pz")
+        mm([(pl(px, 0), I(), fp), (pz, B(), fu)], True, False)
+        mm([(pl(px, 0), I(), pl(E, d)) for d in range(3)], False, True)
+        pc = tt(m("pc"), P, pl(px, 0), AL.is_gt)
+        u = act(m("u"), Q, AF.Exp, kcol(AQ, -AQ * (9 + 113.5)), -AQ)
         tP = m("tP", n=3 * HW)
         for d in range(3):
+            names[("tb", pl(tP, d)[1])] = "tP%d" % d
             tt(pl(tP, d), pl(E, d), pc, AL.mult)
-        pm = bank(x, "a", 1, 3)
+        pm = at("pm", 3)
         mm([(pm, B(), tP)])
         st = act(m("st", n=3 * HW), pm, AF.Sign, kcol(-EPS, -1.5 * EPS))
-        pcn = bank(x, "a", 4)
+        pcn = at("pcn")
         mm([(pcn, D15, one)] + [(pcn, DM, pl(st, d)) for d in range(3)])
-        tw = tt(m("t"), u, pcn, AL.min)
-        p2, p2j = bank(x, "a", 5), bank(x, "b", 7)
+        tw = tt(m("tw"), u, pcn, AL.min)
+        p2 = at("p2")
         mm([(p2, TINY, P), (p2, IB, tw)])
-        mm([(p2j, IB, tw)])
-        zn = act(m("Zn"), px, AF.Relu, 1.0, -64.0)
-        pz = bank(x, "b", 0)
-        mm([(pz, B(), fs)])
-        zf = act(m("Zf"), pz, AF.Relu, -15.0)
-        pw = bank(x, "b", 3, 3)
-        mm([(il(pw, d), I(), pl(E, d)) for d in range(3)] + [(il(pw, 0), I(4), zn), (il(pw, 0), I(4), zf)])
-        w = tt(m("w", "tf", 3 * HW), dk, pw, AL.min)
-        gg = act(m("gg", n=3 * HW), pw, AF.Sign, -0.5)
-        cl = il(scan(m("cl", "tf", 3 * HW), keep3, w), 2)
-        cc = ts(m("cc", "ti"), ts(m("ci", "ti"), cl, 2.0 ** 19, AL.mult), 4095, AL.bitwise_and)
-        nn = ts(m("nn", "ti"), ts(m("ni", "ti"), N, float(ROT - 32), AL.add), 4095, AL.bitwise_and)
-        Pp = ts(m("Pp"), p2, 0.0, AL.is_gt)
-        js = act(m("Js"), p2j, AF.Sign, -2.0 ** -110, 1.0, s["cnt"] if t < NV - 1 else None)
-        cP = tt(m("cP", "tf"), cc, Pp, AL.mult)
-        pcv = bank(x, "a", 7)
-        mm([(pcv, blk32, cP)])
-        pum = bank(x, "a", 4)
-        mm([(pum, I(-1024), fs), (pum, IBm(2048.0, 1024.0), Pp)])
-        pct = bank(x, "a", 1)
-        mm([(pct, I(), DG1), (pct, blk32, cP)])
-        pr = tt(m("pr", "ti"), nn, pcv, AL.mult)
-        xi = ts(m("xi", "ti"), pr, 5, AL.arith_shift_right, 2047, AL.bitwise_and)
-        off = ts(m("off", "tu"), tt(m("xo", "tf"), xi, pum, AL.max), 2048.0, AL.min)
+        z = act(m("z", n=2 * HW), px, AF.Relu, 8.0, -512.0)
+        pA = at("pA", 3)
+        mm([(pl(pA, e, 3 - e), I(), pl(E, 0, 3 - e)) for e in range(3)], True, False)
+        mm([(pl(pA, d), I(), pl(z, e)) for d in range(3) for e in range(2)], False, True)
+        gg = act(m("gg", n=3 * HW), pA, AF.Sign, -0.5)
+        pd = tt(m("pd", "th16", 3 * HW), gg, f["dl"], AL.mult)
+        pcc = at("pcc")
+        mm([(pcc, H16, f["c0"])] + [(pcc, H16, pl(pd, d)) for d in range(3)])
+        nn = ts(m("nn", "ti"), N, 4095, AL.bitwise_and)
+        Pp = ts(m("Pp%d" % t) if t else s["P0"], p2, 0.0, AL.is_gt)
+        names[(Pp[0], Pp[1])] = "Pp"
+        if t == 0:
+            send(s["HP"], state(1)["HP"], 1, "seth")
+        cnt = m("cnt", "tf", 1)
+        if t < NV - 1:
+            act(m("js"), p2, AF.Sign, -2.0e-32, 1.0, cnt)
+        cP = tt(m("cP", "th16"), Pp, pcc, AL.mult)
+        pcv = at("pcv")
+        mm([(pcv, I(8192), fu), (pcv, IBm(8160.0, 2080.0), Pp), (pcv, B16, cP)])
+        pct = at("pct")
+        mm([(pct, I(), DG1), (pct, B(3232), Pp), (pct, B16, cP)])
+        pr = m("pr", "ti", HW + 8)
+        names[("ti", pr[1] + 8)] = "pre"
+        tt(sub(pr, 8, HW + 8), nn, pcv, AL.mult)
         sc = scan(m("sc", "tf"), sub(keep, 0, HW), pct)
-        c1 = ts(m("c1", "ti", 4), sub(sc, 15, HW, 16), float(ROT - 32), AL.add)
-        c3 = cp(m("c3", "tu", 4), ts(m("c2", "ti", 4), c1, 2047, AL.bitwise_and))
-        xc = gather("S", m("xc"), XG, c3)
-        y, ad = m("y", n=16 * HW), m("ad", n=16 * HW)
+        ts(sub(pr, 0, 8), sub(sc, 15, HW, 16), 32.0, AL.mult)
+        xi = ts(m("xi", "ti", HW + 8), pr, 5, AL.arith_shift_right, 2047 + (255 << 18), AL.bitwise_and)
+        off = ts(m("off", "tu", HW + 8), xi, 2048.0, AL.min)
+        xy, ad, ys = m("xy", n=17 * HW), m("ad", n=16 * HW), m("ys", n=16 * HW)
+        xc, y = pl(xy, 0), pl(xy, 1, 16)
         for (e_, a, b) in PAR["gather"]:
-            gather(e_, sub(y, 16 * a, 16 * b), XG, sub(off, a, b))
-        for c in range(2):
-            pdd = tl("pb%d" % (2 + c), 0, 512)
-            mm([(pl(pdd, k), ident, xc) for k in range(8)], True, False)
-            mm([(pl(pdd, k), I(-1), sub(y, 8 * c + k, 16 * HW, 16)) for k in range(8)], False, True)
+            names[("tb", xy[1] + 16 * a)] = "y%d" % a
+            gather(e_, sub(xy, 16 * a, 16 * b), X["g"], sub(off, a, b))
+        kps = ts(m("kps"), cP, -0.5, AL.is_lt, 0.5, AL.subtract)
+        pD = at("pD")
+        mm([(pD, I(8192), fu), (pD, I(8192), Pp), (pD, B(-131072), kps)], True, False)
+        for c in range(4):
+            x, k0_ = c // 2, 8 * (c % 2)
+            pdd = tl("pb%d" % (c % PAR["ring"]), 0, 512)
+            names[(pdd[0], 0)] = "pdd%d" % c
+            names[("tb", ad[1] + 512 * c)] = "ad%d" % c
+            names[("tb", ys[1] + 512 * c)] = "ys%d" % c
+            mm([(sub(pdd, 64 * k, 64 * k + 64), ident, sub(xc, 64 * x, 64 * x + 64)) for k in range(8)], True, False)
+            mm([(sub(pdd, 64 * k, 64 * k + 64), I(-1), sub(y, 1024 * x + k0_ + k, 1024 * x + 1024, 16)) for k in range(8)], False, True)
             act(sub(ad, 512 * c, 512 * c + 512), pdd, AF.Abs)
-        kps = act(m("KPs"), cP, AF.Sign, -16.0)
-        pD = bank(x, "a", 0)
-        lanes = [(pD, sub(SEL, 15 - k, 143 - k), pl(ad, k)) for k in range(16)]
-        mm([(pD, I(-4096), fs), (pD, I(8192), Pp), (pD, B(-4096), kps)] + lanes[:8], True, False)
-        mm(lanes[8:], False, True)
-        pq = bank(x, "b", 1)
-        pd = act(m("Pd"), Q, AF.Relu, -8.0, -1.0)
-        qn = ts(m("Qn"), Q, -8.0, AL.max)
-        mm([(pq, I(-1), pd), (pq, I(-8), js), (pq, IBm(-512.0, 496.0), Pp)])
-        tt(Q, qn, pq, AL.min)
-        pt2 = bank(x, "b", 6)
+            mm([(sub(pD, 64 * x, 64 * x + 64), sub(SEL, 15 - k0_ - k, 143 - k0_ - k), sub(ad, 512 * c + 64 * k, 512 * c + 64 * k + 64))
+                for k in range(8)], False, c == 3)
+            scan(sub(ys, 512 * c, 512 * c + 512), keep, sub(y, 512 * c, 512 * c + 512))
+        ts(Q, Q, 8.0, AL.min)
+        pt2 = at("pt2")
         mm([(pt2, I(), tw), (pt2, I(-BIG), Pp)])
         t2 = act(m("t2"), pt2, AF.Relu)
-        p3 = bank(x, "b", 7)
+        p3 = at("p3")
         mm([(p3, IB, t2)])
         if "J2" in onS:
             j2, jm, jb = act(m("J2"), p3, AF.Sign, -2.0 ** -110), scaled(BK, 0.5), 0.59375
         else:
             j2, jm, jb = ts(m("J2"), p3, 0.0, AL.is_gt), BK, 0.0
-        pR = bank(x, "b", 2, 4)
-        mm([(pl(pR, d), BK, Pp) for d in range(4)])
-        eq = tt(m("eq", n=4 * HW), HE, pR, AL.is_equal)
-        pcm = bank(x, "b", 6)
-        mm([(pcm, I(pa), P), (pcm, I(6), zn), (pcm, I(6), zf), (pcm, I(4), js), (pcm, jm, j2)])
-        cm = act(m("cm"), pcm, AF.Identity, -6.0 + pb + jb)
-        prs = bank(x, "b", 2, 4)
-        pe3 = sub(prs, HW, 4 * HW)
-        mm([(pl(prs, 0), I(), pl(eq, 0)), (pl(prs, 0), I(), Pp), (pe3, I(12), sub(eq, HW, 4 * HW)), (pe3, I(-2), E)]
-           + [(pl(pe3, d), I(), cm) for d in range(3)])
-        tt(HE, HE, prs, AL.max)
-        pup = bank(x, "b", 1)
+        pR = at("pR", 3)
+        mm([(pl(pR, d), BK, Pp) for d in range(3)])
+        eq = tt(m("eq", n=3 * HW), E, pR, AL.is_equal)
+        pcm = at("pcm")
+        mm([(pcm, I(), pl(z, 0)), (pcm, I(), pl(z, 1)), (pcm, I(16), Pp), (pcm, jm, j2)])
+        cm = act(m("cm"), pcm, AF.Identity, -17.0 + jb)
+        prs = at("prs", 4)
+        pe3, pq = pl(prs, 0, 3), pl(prs, 3)
+        mm([(pe3, I(-1), E), (pq, I(), fu), (pq, I(-8 if "P" in onS else -16), P), (pq, IBm(512.0, -496.0), Pp)], True, False)
+        mm([(pe3, I(256), eq)], False, False)
+        mm([(pl(pe3, d), I(), cm) for d in range(3)], False, True)
+        tt(EQ, EQ, prs, AL.max)
+        pup = at("pup")
         mm([(pup, I(), u), (pup, I(-BIG), Pp)])
         up = act(m("up"), pup, AF.Relu)
-        pY = bank(x, "b", 7)
+        pY = at("pY")
         mm([(pY, IB, up)])
         if "nq" in onS:
-            pn = bank(x, "b", 1)
-            mm([(pn, I(), fp), (pn, I(256), act(m("Yh"), pY, AF.Sign))])
-            nq = act(m("nq"), pn, AF.Relu, -256.0)
+            pn = at("pn")
+            mm([(pn, I(), fp), (pn, I(2048), act(m("Yh"), pY, AF.Sign))])
+            nq = act(m("nq"), pn, AF.Relu, -512.0, 0.25)
         else:
-            nq = tt(m("nq"), ts(m("Yh"), pY, 0.0, AL.is_gt), fp, AL.mult)
-        U = bank(x, "u", 0, 5)
-        ub = [pl(U, i) for i in range(5)]
-        mm([(ub[d], I(-8), il(gg, d)) for d in range(3)]
-           + [(ub[1], I(8), il(gg, 0)), (ub[2], I(8), il(gg, 0)), (ub[2], I(8), il(gg, 1))], True, False)
-        mm([(ub[4], key32, cl)], False, False)
-        mm([(ub[0], IBm(-16.0, 23.0), Pp), (ub[1], IBm(-16.0, 31.0), Pp), (ub[2], IBm(-16.0, 39.0), Pp), (ub[3], QK, Pp),
-            (ub[4], I(16384 * (t - 31)), Pp)], False, False)
-        mm([(ub[3], I(192), kps), (ub[4], I(2 ** 19), kps)], False, False)
-        mm([(ub[3], B(), nq)], False, False)
-        if t not in thrs:
-            mt = tmpf(2)
-            pt = sub(bank(x, "b", 7), 0, 1)
-            mm([(pt, ones32, slot(t, 0)["old"]), (pt, ones32, slot(t, 1)["old"])])
-            a7 = ts(mt("a7", "ti", 1), ts(mt("tot", "ti", 1), pt, 0.5, AL.mult), 7, AL.bitwise_and)
-            thrs[t] = ts(mt("thr%d" % t, "tf", 1), a7, 32.0 * TS, AL.mult, thp, AL.add)
-        if "cf" in onS:
-            tO = tt(m("tO"), act(m("cf"), pD, AF.Relu, thrs[t], -TS), r, AL.min)
-        else:
-            tO = tt(m("tO"), ts(m("cf"), pD, thrs[t], AL.is_le), r, AL.mult)
-        p4 = bank(x, "a", 4)
+            nq = tt(m("nq"), ts(m("Yh"), pY, 0.0, AL.is_gt, 0.25, AL.mult), fp, AL.mult)
+        U, UQ = at("U", 3), at("UQ")
+        ub = [pl(U, i) for i in range(3)]
+        mm([(U, I(-8), gg), (pl(U, 1, 2), I(8), pl(gg, 0, 2))], True, False)
+        mm([(ub[0], IBm(-16.0, 23.0), Pp), (ub[1], IBm(-16.0, 31.0), Pp), (ub[2], IBm(-16.0, 31.0), Pp)], False, False)
+        mm([(UQ, QK, Pp), (UQ, I(-384), kps), (UQ, B(-1), nq)], True, False)
+        thr = ts(m("thr", "tf", 1), s["a7"], 16.0, AL.mult, thp, AL.add) if t else thp
+        cf = ts(m("cf"), pD, thr, AL.is_le, 131072.0, AL.mult)
+        mm([(UQ, B(), cf)], False, True)
+        tt(Q, Q, UQ, AL.min)
+        if t == 0:
+            send(Q, state(1)["Q"], 1, "setq")
+        tO = tt(m("tO"), cf, r, AL.mult)
+        p4 = at("p4")
         mm([(p4, IB, tO)])
         O = ts(m("O"), p4, 0.0, AL.is_gt)
-        mm([(ub[0], BK1, O), (ub[1], BK1, O), (ub[2], BK1, O), (ub[3], B(-384), O), (ub[4], B(-2 ** 20), O)], False, True)
-        tt(E, E, sub(U, 0, 3 * HW), AL.min)
-        tt(Q, Q, ub[3], AL.max)
-        tt(N, N, ub[4], AL.max)
-        if t < NV - 1:
-            n = slot(t + 1, x)
-            for j, z in enumerate(["lb", "lf"]):
-                i = add("G", "send", (s[z], n[z], 4 * t + 2 * x + j), [s[z]], [], PAR["issue"])
-                add(None, "recv", (4 * t + 2 * x + j,), [], [n[z]], PAR["flight"], [i])
-        for c in range(2):
-            scan(sub(m("ys"), 512 * c, 512 * c + 512), keep, sub(y, 512 * c, 512 * c + 512))
+        mm([(ub[0], BK1, O), (ub[1], BK1, O), (ub[2], BK1, O)], False, True)
+        tt(E, E, U, AL.min)
+        pN = at("pN")
+        mm([(pN, I16, cP), (pN, I(2048), pl(gg, 0)), (pN, I(2048), pl(gg, 1)), (pN, I(7328), Pp), (pN, I(32768 * (t + 1)), kps),
+            (pN, B(-1), cf)])
+        tt(N, N, pN, AL.max)
+        if t == 0:
+            send(E, state(1)["E"], 1, "sete")
+        Y = sub(ys, 15, 16 * HW, 16)
+        msg = tl("mo", 144 * t, 144 * t + HW + 8)
+        pv = at("pv")
+        mm([(pv, I(0.5), xc), (pv, I(0.5), Y)])
+        ts(sub(msg, 0, HW), pv, -0.25, AL.add)
+        ns = 9 if t < NV - 1 else 8
+        ph = sub(at("ph", 2), 0, 16 * ns)
+        mm([(ph, I(), sub(DG2, 0, 16 * ns))] + ([(sub(ph, 143, 144), ones32, cnt)] if ns == 9 else [])
+           + [(pl(ph, 0), B(-131072), kps), (pl(ph, 0), BW, Y), (pl(ph, 0), B(), cf)])
+        sh = scan(sub(m("sh", "tf", 144), 0, 16 * ns), sub(keep, 0, 16 * ns), ph)
+        h1 = cp(sub(m("h1", "ti", 9), 0, ns), sub(sh, 15, 16 * ns, 16))
+        h2 = ts(sub(s["h2"], 0, ns), h1, (31 << 17) + 15, AL.bitwise_and)
+        h3 = ts(m("h3", "tf", 8), sub(h2, 0, 8), 2064.0, AL.min)
+        cp(sub(msg, HW, HW + 8), tt(m("h4", "tf", 8), h3, bases, AL.add))
+        if t == 0:
+            send(s["li"], state(1)["li"], 1, "seti")
+        if 0 < t < NV - 1:
+            land = tl("mi", 144 * t, 144 * t + HW + 8)
+            send(msg, land, -1, "new")
+            scatter(table(t + 1)["w"], land)
+        else:
+            scatter(X["w"], msg)
 
-    def table():
-        m = tmpf(2)
-        Y = sub(both["ys"], 15, 32 * HW, 16)
-        pv = tl("pb2", 0, 128)
-        mm([(pv, I(0.5), both["xc"]), (pv, I(0.5), Y)])
-        vi = ts(m("vi", "ti", 128), pv, -0.25, AL.add)
-        ph = tl("pb3", 0, 128)
-        mm([(ph, I(), DG2), (ph, BW, Y), (ph, B(-65536), both["KPs"]), (ph, B(131072), both["O"])])
-        sc = scan(m("sc", "tf", 128), sub(keep, 0, 128), ph)
-        h1 = cp(m("h1", "ti", 8), sub(sc, 15, 128, 16))
-        h2 = ts(m("h2", "ti", 8), h1, 131072 + 15, AL.bitwise_and)
-        h3 = ts(m("h3", "tf", 8), h2, 2064.0, AL.min)
-        h5 = cp(m("h5", "tu", 8), tt(m("h4", "tf", 8), h3, bases, AL.add))
-        add("V", "sca", (XW, h5, vi), [h5, vi], [XW], 128 * PAR["sca"] * PAR["cyc"] + 50.0)
-
-    def decode(x):
-        s, m = slot(NV - 1, x), tmpf(x)
-        c0 = x * HW
-        ni = cp(m("ni", "ti"), s["N"])
-        ts(tl("of", c0, c0 + HW), ts(m("nn", "ti"), ni, 4095, AL.bitwise_and), -32.0, AL.add)
-        ts(tl("ob", 128 + c0, 128 + c0 + HW), ts(m("cc", "ti"), ni, 12, AL.arith_shift_right, 3, AL.bitwise_and), -1.0, AL.mult, 2.0, AL.add)
-        tt(tl("ob", c0, c0 + HW), ts(m("r"), s["Q"], kcol(1, -9), AL.add, -1.0, AL.max), ts(m("u"), s["Q"], -8.0, AL.is_lt), AL.subtract)
-        pw = bank(x, "a", 1, 3)
-        mm([(pw, I(-4), sub(ones, 0, 3 * HW)), (pw, I(-4), s["E"])] + [(pl(pw, d), I(), s["H"]) for d in range(3)])
+    def decode():
+        s = state(NV - 1)
+        ts(tl("of", 0, HW), ts(m("nn", "ti"), s["N"], 4095, AL.bitwise_and), -float(ROT), AL.add)
+        ts(tl("ob", 128, 256), ts(m("n2", "ti"), s["N"], 12, AL.arith_shift_right, 3, AL.bitwise_and), -1.0, AL.mult, 2.0, AL.add)
+        tt(tl("ob", 0, HW), ts(m("r"), s["Q"], -1.0, AL.mult, kcol(1, -9), AL.add),
+           ts(m("u"), s["Q"], 16.0, AL.is_le, 2.0, AL.subtract), AL.max)
+        pe, pM, pH = at("pe"), at("pM"), at("pH")
+        mm([(pe, I(), s["P0"])] + [(pe, I(), m("Pp%d" % t)) for t in range(1, NV)])
+        ev = ts(m("ev"), pe, 0.0, AL.is_gt)
+        mm([(pM, B2k, ev)])
+        fx = tt(m("fx"), act(m("f1"), s["H"], AF.Exp, 17 * LN2, -128 * LN2), ts(m("f2"), s["H"], 2.0 ** 22, AL.mult), AL.min)
+        bit = ts(m("b2", "ti"), tt(m("b1", "ti"), fx, pM, AL.mult), 15, AL.arith_shift_right, 1, AL.bitwise_and)
+        mm([(pH, I(), s["H"]), (pH, I(), ev), (pH, I(), cp(m("b3"), bit))])
+        H = act(m("H"), pH, AF.Identity)
+        pw = at("pw", 3)
+        mm([(pw, I(-8), ones), (pw, I(-8), s["E"])] + [(pl(pw, d), I(), H) for d in range(3)])
         e1 = tt(m("tP", n=3 * HW), s["E"], pw, AL.max)
         xx = ts(m("st", n=3 * HW), e1, 1.0, AL.min, 128.0, AL.mult)
         sg = act(m("gg", n=3 * HW), e1, AF.Sign, -0.5)
-        po = bank(x, "a", 5, 3)
+        po = at("po", 3)
         mm([(po, I(), xx), (po, I(-63.5), sg)])
         for d in range(3):
-            act(tl("ob", 256 + 3 * c0 + d, 256 + 3 * c0 + 3 * HW, 3), pl(po, d), AF.Identity, -65.5)
+            act(tl("ob", 256 + d, 640, 3), pl(po, d), AF.Identity, -65.5)
 
-    for x in range(2):
-        lead[0], lead[1] = PAR["lead0"] * (1 - x), 0
-        encode(x)
+    phase[0] = 0
+    encode()
     for t in range(NV):
-        lead[1] = 0 if t == 0 else (2 if t == NV - 1 else 1)
-        for x in range(2):
-            lead[0] = PAR["lead" if t else "lead0"] * (1 - x)
-            visit(t, x)
-        table()
-    decode(0)
-    decode(1)
-    dma("Y", tl("yx", 0, 2048 - ROT), tl("xw", ROT, 2048))
-    dma("S", tl("yx", 2048 - ROT, 2048), tl("xw", 0, ROT))
+        phase[0] = 0 if t == 0 else (2 if t == NV - 1 else 1)
+        visit(t)
+    decode()
+    b = table(NV - 1)["x"]
+    dma("Y", tl("yx", 0, 2048 - ROT), sub(b, ROT, 2048))
+    dma("S", tl("yx", 2048 - ROT, 2048), sub(b, 0, ROT))
     dma("Y", tl("yn", 0, 128), tl("of", 0, 128))
     dma("Y", tl("yp", 0, 128), tl("ob", 0, 128))
     dma("Y", tl("yd", 0, 128), tl("ob", 128, 256))
     dma("Y", tl("yg", 0, 384), tl("ob", 256, 640))
+    assert narr[0] == NARR
     return ops
 
 
@@ -504,7 +558,7 @@ def schedule(ops, shift):
     prio = [0.0] * n
     for i in range(n - 1, -1, -1):
         prio[i] = lat[i] + max([prio[j] + PAR["cross"] for j in succ[i]] + [0.0])
-    rank_ = [prio[i] + o["lead"] + shift.get(o["role"], 0.0) for i, o in enumerate(ops)]
+    rank_ = [prio[i] + shift.get(o["role"], 0.0) for i, o in enumerate(ops)]
     for i in range(n - 1, -1, -1):
         if ops[i]["const"] and succ[i]:
             rank_[i] = lat[i] + PAR["cross"] + max(rank_[j] for j in succ[i]) + shift.get(ops[i]["role"], 0.0)
@@ -605,6 +659,100 @@ def search(ops):
     return schedule(ops, kept)
 
 
+def place(ops, pred, low, prio):
+    n = len(ops)
+    succ = [[] for _ in ops]
+    left = [len(pred[i]) for i in range(n)]
+    for i in range(n):
+        for j, _w in pred[i]:
+            succ[j].append(i)
+    heap = sorted((-prio[i], i) for i in range(n) if not left[i])
+    start = [0.0] * n
+    busy = {}
+    gap = PAR["cross"]
+    while heap:
+        i = heap.pop(0)[1]
+        o = ops[i]
+        t = max([low[i]] + [start[j] + w for j, w in pred[i]])
+        c, e = o["cost"], o["eng"]
+        res = [(e, 0.0)] + [(b, gap) for b in o["banks"]] if e else []
+        moved = True
+        while moved:
+            moved = False
+            for r, g_ in res:
+                lst = busy.get(r, ())
+                k = len(lst) - 1
+                while k >= 0 and lst[k][0] > t - 2500.0:
+                    k -= 1
+                for a, b, e2 in lst[k + 1:]:
+                    if a - g_ >= t + c:
+                        break
+                    if b + g_ > t and (g_ == 0.0 or e2 != e):
+                        t = b + g_
+                        moved = True
+        start[i] = t
+        for r, _g in res:
+            lst = busy.setdefault(r, [])
+            k = len(lst)
+            while k and lst[k - 1][0] > t:
+                k -= 1
+            lst.insert(k, (t, t + c, e))
+        for j in succ[i]:
+            left[j] -= 1
+            if not left[j]:
+                k = len(heap)
+                while k and heap[k - 1][0] > -prio[j]:
+                    k -= 1
+                heap.insert(k, (-prio[j], j))
+    return start
+
+
+def search(ops):
+    n = len(ops)
+    cost = [o["cost"] for o in ops]
+    lat = [o["cost"] + (PAR["dma"] if o["kind"] == "dma" else 0.0) for o in ops]
+    fwd, bwd = [[] for _ in ops], [[] for _ in ops]
+    for i, o in enumerate(ops):
+        for j in o["deps"]:
+            e = ops[j]["eng"]
+            w = lat[j] + (0.0 if e == o["eng"] == "P" else PAR["same"] if e == o["eng"] else PAR["cross"])
+            fwd[i].append((j, w))
+            bwd[j].append((i, w + cost[i] - cost[j]))
+    zero, tail = [0.0] * n, [lat[i] - cost[i] for i in range(n)]
+    seed = [PAR["seed"]]
+
+    def rnd():
+        seed[0] = (seed[0] * 1103515245 + 12345) % 2147483648
+        return seed[0] / 2147483648.0
+    prio = [0.0] * n
+    for i in range(n - 1, -1, -1):
+        prio[i] = max([tail[i]] + [prio[j] + w for j, w in bwd[i]])
+    prio = [prio[i] + cost[i] for i in range(n)]
+    best, cur = None, None
+    for it in range(PAR["iters"]):
+        s = place(ops, fwd, zero, prio)
+        r = place(ops, bwd, tail, [s[i] + cost[i] for i in range(n)])
+        back = [r[i] + cost[i] for i in range(n)]
+        s = place(ops, fwd, zero, back)
+        v = max(s[i] + lat[i] for i in range(n))
+        if best is None or v < best[0]:
+            best = (v, s)
+        if cur is None or v <= cur[0] + PAR["slack"] * rnd() * (1.0 - it / PAR["iters"]):
+            cur = (v, back)
+        shake = {}
+        prio = [cur[1][i] + shake.setdefault(ops[i]["role"], (rnd() - 0.5) * PAR["step"] if rnd() < PAR["share"] else 0.0) for i in range(n)]
+    order = sorted(range(n), key=lambda i: (best[1][i], i))
+    last = {}
+    for i in order:
+        o = ops[i]
+        o["start"] = best[1][i]
+        o["waits"] = set(o["deps"])
+        for b in o["banks"]:
+            o["waits"].update(j for e, j in last.get(b, {}).items() if e != o["eng"])
+            last.setdefault(b, {})[o["eng"]] = i
+    return order, best[0]
+
+
 PLAN = {}
 
 
@@ -616,16 +764,15 @@ def rank_program(g, core, T, topo):
         PLAN["ops"] = build()
         PLAN["order"] = search(PLAN["ops"])[0]
     ops, order = PLAN["ops"], PLAN["order"]
-    nxt = T.cores[(rank + 1) % len(T.cores)]
-    rid, pid = topo.addr(nxt, core)
-    eng = topo.engines(core, nxt)
-    he = len(eng) // 2
     queue = {"V": g.vector, "S": g.scalar, "P": g.tensor, "G": g, "Y": g.sync}
     count = {}
     token = {}
     clock = {}
     known = {k: {} for k in queue}
     ndma = [0]
+
+    def peer(hop):
+        return T.cores[(rank + hop) % len(T.cores)]
 
     def ap(t):
         if not isinstance(t, tuple):
@@ -643,14 +790,15 @@ def rank_program(g, core, T, topo):
         o = ops[i]
         e, kind, a = o["eng"], o["kind"], o["args"]
         if kind == "recv":
-            token[i] = ("arr%d" % a[0], 2 * he)
-            count[token[i][0]] = 2 * he
-            clock[i] = {token[i][0]: 2 * he}
+            n = sum(len(topo.engines(peer(-h), core)) for h in ops[a[1]]["args"][3])
+            token[i] = ("arr%d" % a[0], n)
+            count[token[i][0]] = n
+            clock[i] = {token[i][0]: n}
             continue
         q, kn = queue[e], known[e]
         need = {}
         for j in o["waits"]:
-            if e == "P" and ops[j]["eng"] == "P":
+            if (e == "P" and ops[j]["eng"] == "P") or ops[j]["kind"] == "send":
                 continue
             s_, v = token[j]
             if v > need.get(s_, (0, 0))[0]:
@@ -661,8 +809,15 @@ def rank_program(g, core, T, topo):
                 for k_, v_ in clock[j].items():
                     kn[k_] = max(kn.get(k_, 0), v_)
         if kind == "send":
-            g.remote_dma(ap(a[1]), ap(a[0]), T.sem["arr%d" % a[2]], T.sem.sent, pid, rid, topo.mask(core, nxt))
-            count["sent"] = count.get("sent", 0) + 2 * he
+            dst = peer(a[3][0])
+            to = [topo.addr(peer(h), core) for h in a[3]]
+            if len(to) == 1:
+                g.remote_dma(ap(a[1][0]), ap(a[0]), T.sem["arr%d" % a[2]], T.sem.sent, to[0][1], to[0][0], topo.mask(core, dst))
+            else:
+                g.remote_dma_fused([RemoteDMATransfer(dst_ids=[DstId(rid=r_, pnc=p_) for r_, p_ in to], dma_engine_mask=topo.mask(core, dst),
+                                                      remote_sem=T.sem["arr%d" % a[2]], srcs=[ap(a[0])], dsts=[ap(d_) for d_ in a[1]])],
+                                   local_sem=T.sem.sent)
+            count["sent"] = count.get("sent", 0) + len(topo.engines(core, dst))
             continue
         if kind == "ts":
             if a[5] is None:
@@ -674,7 +829,7 @@ def rank_program(g, core, T, topo):
         elif kind == "cp":
             ins = q.tensor_copy(ap(a[0]), ap(a[1]))
         elif kind == "fill":
-            ins = q.memset(ap(a[0]), a[1])
+            ins = q.memset(ap(a[0]), int(a[1]) if SCRATCH[a[0][0]][2] == "int32" else a[1])
         elif kind == "scan":
             ins = q.tensor_tensor_scan(ap(a[0]), ap(a[1]), ap(a[2]), 0.0, AL.mult, AL.max)
         elif kind == "act":

from concourse.bass import DstId, RemoteDMATransfer
from concourse.mybir import AluOpType, ActivationFunctionType

HW = 128
NV = 6
ROT = 1184
XC = 4112
ST = 528
SCRATCH = {
    "cb": ("sbuf", [128, 12288], "bfloat16"),
    "ch": ("sbuf", [128, 512], "float16"),
    "cf": ("sbuf", [128, 1024], "float32"),
    "tb": ("sbuf", [128, 16384], "bfloat16"),
    "th16": ("sbuf", [128, 1024], "float16"),
    "tf": ("sbuf", [128, 2048], "float32"),
    "ti": ("sbuf", [128, 3072], "int32"),
    "tu": ("sbuf", [128, 256], "uint16"),
    "xw": ("sbuf", [128, 5 * XC], "bfloat16"),
    "lb": ("sbuf", [128, 2 * 768], "bfloat16"),
    "li": ("sbuf", [128, 2 * 144], "int32"),
    "ls": ("sbuf", [128, 4 * ST], "float16"),
    "mo": ("sbuf", [128, NV * 144], "uint16"),
    "mi": ("sbuf", [128, NV * 144], "uint16"),
    "inb": ("sbuf", [128, 640], "bfloat16"),
    "ini": ("sbuf", [128, 528], "int32"),
    "ob": ("sbuf", [128, 640], "bfloat16"),
    "of": ("sbuf", [128, 128], "float32"),
}
for _b in range(8):
    SCRATCH["pb%d" % _b] = ("psum", [128, 512], "float32")
NDMA = 16
NARR = 13
SEMAPHORES = ["qV", "qS", "qP", "qG", "sent"] + ["arr%d" % i for i in range(NARR)] + ["dma%d" % i for i in range(NDMA)]

AL, AF = AluOpType, ActivationFunctionType
WIDE = {"float32": 4, "int32": 4, "bfloat16": 2, "uint16": 2, "float16": 2}
PAR = {"cyc": 1.0, "pe": 0.5, "vfix": 30.0, "sfix": 65.0, "same": 60.0, "cross": 100.0, "gat": 1.56, "sca": 3.5,
       "issue": 1000.0, "flight": 2000.0, "rate": 80.0, "after": ["seth", "setq"], "dma": 2200.0, "seed": 1, "iters": 1500, "step": 3000.0,
       "slack": 300.0, "share": 0.03,
       "gather": [("S", 0, 24), ("V", 24, 72), ("S", 72, 104), ("V", 104, 136)],
       "onS": "P J2 nq", "turn": 2, "ring": 3,
       "onG": [0.5, 16, 256, 8, -8, 2048, 7328, -384, -63.5] + [32768 * (t + 1) for t in range(NV)]}
AT = {"p1": (4, 0), "px": (5, 0), "pz": (5, 1), "pA": (6, 0), "pm": (7, 0), "pcn": (4, 1), "p2": (5, 2), "p2j": (6, 3),
      "pcc": (7, 3), "pcv": (4, 2), "pct": (5, 3), "pD": (4, 0), "pq": (5, 0), "pt2": (6, 0), "p3": (7, 0), "pR": (5, 0),
      "pcm": (6, 1), "prs": (7, 0), "pup": (6, 2), "pY": (6, 3), "pn": (5, 0), "pt": (6, 0), "U": (3, 0), "pN": (5, 1),
      "p4": (4, 1), "pv": (6, 0), "ph": (7, 0), "enc": (6, 0), "pw": (6, 0), "po": (7, 0),
      "pe": (5, 0), "pM": (6, 0), "pH": (5, 1)}
AT.update({"pA": (0, 0), "p2j": (2, 3), "pm": (1, 0), "p2": (1, 3), "px": (2, 0), "pz": (2, 1), "pcn": (2, 2), "p1": (6, 3),
           "U": (3, 0), "pD": (4, 0), "pcc": (4, 1), "pcv": (4, 2), "pct": (6, 2), "pR": (6, 0), "UQ": (5, 0), "pt2": (5, 1),
           "p3": (5, 2), "pcm": (6, 3), "pup": (5, 1), "pY": (5, 2), "pn": (5, 3), "prs": (7, 0), "pN": (6, 0), "p4": (0, 0),
           "pv": (1, 0), "ph": (2, 0)})


def tl(buf, a, b, step=1, parts=128):
    return (buf, a, b, step, parts)


def sub(t, a, b, step=1):
    return (t[0], t[1] + a, t[1] + b, step, t[4])


def nel(t):
    return (t[2] - t[1] + t[3] - 1) // t[3]


def width(t):
    return WIDE[SCRATCH[t[0]][2]]


def psum(t):
    return t[0][:2] == "pb"


def build():
    ops = []
    top = {}
    acc = {}
    names = {}
    phase = [-1]

    def new(buf, n, parts=128):
        a = top.get(buf, 0)
        top[buf] = a + (n + 15) // 16 * 16
        assert top[buf] <= SCRATCH[buf][1][1], buf
        return tl(buf, a, a + n, 1, parts)

    def add(eng, kind, args, reads, writes, cost, extra=(), tag=None):
        i = len(ops)
        deps = set(extra)
        for t in reads:
            for (a, b, j, w) in acc.get(t[0], []):
                if w and a < t[2] and t[1] < b:
                    deps.add(j)
        for t in writes:
            for (a, b, j, w) in acc.get(t[0], []):
                if a < t[2] and t[1] < b:
                    deps.add(j)
        for t in writes:
            if t[3] == 1:
                acc[t[0]] = [r for r in acc.get(t[0], []) if not (t[1] <= r[0] and r[1] <= t[2])]
            acc.setdefault(t[0], []).append((t[1], t[2], i, True))
        for t in reads:
            acc.setdefault(t[0], []).append((t[1], t[2], i, False))
        deps.discard(i)
        banks = set(t[0] for t in list(reads) + list(writes) if psum(t))
        w0 = (list(writes) + list(reads))[0]
        name = tag or names.get((w0[0], w0[1]), "%s%d" % (w0[0], w0[1] % {"lb": 768, "li": 144, "xw": XC, "mo": 144, "mi": 144}.get(w0[0], 1 << 20)))
        role = (kind, name, len(reads), phase[0])
        ops.append({"role": role, "name": name, "const": w0[0] in ("cb", "cf", "ch") or phase[0] < 0, "eng": eng, "kind": kind,
                    "args": args, "deps": deps, "cost": cost, "banks": banks})
        return i

    def vcost(n):
        return max(64.0, n) * PAR["cyc"] + PAR["vfix"]

    def half(*ts_):
        return 0.5 if all(width(t) == 2 for t in ts_) else 1.0

    def tiles(*xs):
        return [x for x in xs if isinstance(x, tuple)]

    def ts(out, a, s1, op0, s2=None, op1=None):
        add("V", "ts", (out, a, s1, s2, op0, op1), tiles(a, s1, s2), [out], vcost(nel(a) * half(out, a)))
        return out

    def tt(out, a, b, op):
        c = 1.0 if psum(a) or psum(b) else 2.0 * half(out, a, b)
        add("V", "tt", (out, a, b, op), [a, b], [out], vcost(nel(a) * c))
        return out

    def cp(out, a):
        add("V", "cp", (out, a), [a], [out], vcost(nel(a) * half(out, a)))
        return out

    def fill(out, v):
        add("V", "fill", (out, float(v)), [], [out], vcost(nel(out) * half(out)))
        return out

    def scan(out, d0, d1):
        add("V", "scan", (out, d0, d1), [d0, d1], [out], vcost(nel(d1) * half(out, d0, d1)))
        return out

    def act(out, a, fn, bias=0.0, scale=1.0, accum=None, more=0.0):
        add("S", "act", (out, a, fn, bias, scale, accum), tiles(a, bias, scale), tiles(out, accum),
            max(64.0, nel(a)) * PAR["cyc"] + PAR["sfix"] + more)
        return out

    def mm(terms, start=True, stop=True):
        cost = sum(max(64.0, nel(r)) * (4.0 if width(r) == 4 else 1.0) for (_o, _l, r) in terms) * PAR["pe"] + 30.0
        rd = [l for (_o, l, _r) in terms] + [r for (_o, _l, r) in terms]
        wr = [o for (o, _l, _r) in terms]
        if start != stop:
            wr.append(tl(wr[0][0], 0, 512))
        add("P", "mm", (terms, start, stop), rd, wr, cost)

    def gather(eng, out, win, off):
        add(eng, "gat", (out, win, off), [win, off], [out], nel(out) * PAR["gat"] * PAR["cyc"] + 60.0)
        return out

    def scatter(win, msg):
        add("V", "sca", (win, sub(msg, HW, HW + 8), sub(msg, 0, HW)), [msg], [win], HW * PAR["sca"] * PAR["cyc"] + 50.0)

    def dma(eng, out, a):
        add(eng, "dma", (out, a), [a] if a[0] in SCRATCH else [], [out] if out[0] in SCRATCH else [], 100.0)

    narr = [0]
    sends = []

    def send(src, dst, hop, tag):
        if not isinstance(dst, list):
            dst, hop = [dst], [hop]
        i = add("G", "send", (src, dst, narr[0], hop), [src], [], PAR["issue"], sends[-1:] if tag in PAR["after"] else (), tag=tag)
        add(None, "recv", (narr[0], i), [], dst, PAR["flight"] + len(dst) * nel(src) * width(src) * 128 / PAR["rate"], [i], tag=tag)
        sends.append(i)
        narr[0] += 1

    def iota(out, pat, base, cm):
        add("G", "iota", (out, pat, base, cm), [], [out], 130.0 + 2.0 * nel(out))
        return out

    def select(out, a, pat, op, v, cm):
        add("G", "sel", (out, a, pat, op, float(v), cm), [a], [out], 170.0 + 2.0 * nel(out))
        return out

    def table(t):
        b = max(t - 1, 0) * XC
        return {"x": tl("xw", b, b + 2048), "g": tl("xw", b, b + 2064), "w": tl("xw", b, b + XC), "z": tl("xw", b + 2048, b + 2064)}

    ps_in, dv_in, ex_in = tl("inb", 0, 128), tl("inb", 128, 256), tl("inb", 256, 640)
    nm_in, dn_in, wt_in, th_in = tl("ini", 0, 128), tl("ini", 128, 512), tl("ini", 512, 513), tl("ini", 520, 521)
    dma("Y", ps_in, tl("ps", 0, 128))
    dma("S", ex_in, tl("ex", 0, 384))
    dma("Y", dv_in, tl("dv", 0, 128))
    dma("S", dn_in, tl("dn", 0, 384))
    dma("Y", nm_in, tl("nm", 0, 128))
    dma("Y", tl("xw", ROT, 2048), tl("xt", 0, 2048 - ROT))
    dma("Y", tl("xw", 0, ROT), tl("xt", 2048 - ROT, 2048))
    dma("Y", th_in, tl("th", 0, 1))
    dma("Y", wt_in, tl("wt", 0, 1))

    pi_ = iota(new("ti", 1), [[0, 1]], 0, 1)
    col = iota(new("ti", 144), [[1, 144]], 0, 0)
    ki = ts(new("ti", 1), pi_, 15, AL.bitwise_and)
    kf = cp(new("cf", 1), ki)
    pf = cp(new("cf", 1), pi_)
    g16 = tt(new("cf", 1), pf, kf, AL.subtract)
    cache = {}

    def kcol(mul, off):
        if ("k", mul, off) not in cache:
            cache[("k", mul, off)] = ts(new("cf", 1), kf, float(mul), AL.mult, float(off), AL.add)
        return cache[("k", mul, off)]
    col128 = sub(col, 0, 128)
    ident = ts(new("cb", 128), col128, pf, AL.is_equal)
    colg = ts(new("ti", 128), col128, 112, AL.bitwise_and)
    blk = ts(new("cb", 128), colg, g16, AL.is_equal)
    turn = [0]
    zeros = fill(new("cb", 128), 0.0)

    def scaled(base, s):
        key = (base, s)
        if key not in cache:
            turn[0] += 1
            if s == 1:
                cache[key] = base
            elif isinstance(s, tuple) or 1e-20 < abs(s) < 1e20:
                s_ = s if isinstance(s, tuple) else float(s)
                if base == ident and s in PAR["onG"]:
                    cache[key] = select(new("cb", 128), zeros, [[-1, 128]], AL.not_equal, s_, 1)
                elif turn[0] % PAR["turn"] == 0:
                    cache[key] = act(new("cb", 128), base, AF.Identity, 0.0, s_)
                else:
                    cache[key] = ts(new("cb", 128), base, s_, AL.mult)
            else:
                cache[key] = ts(new("cb", 128), base, 2.0 ** 60, AL.mult, float(s / 2.0 ** 60), AL.mult)
        return cache[key]

    def I(s=1):
        return scaled(ident, s)

    def B(s=1):
        return scaled(blk, s)

    def IBm(a, b):
        if ("m", a, b) not in cache:
            cache[("m", a, b)] = select(new("cb", 128), B(b), [[-1, 128]], AL.not_equal, a + b, 1)
        return cache[("m", a, b)]
    BIG = 2.0 ** 120
    LN2 = 0.6931471805599453
    EPS = 1.0 / 128
    IB = IBm(1.0, -0.4)
    ones = fill(new("cb", 3 * HW), 1.0)
    one = sub(ones, 0, HW)
    B16, I16, H16 = cp(new("ch", 128), blk), cp(new("ch", 128), ident), ts(new("ch", 128), ident, 0.5, AL.mult)
    TINY = ts(new("cb", 128), ident, 2.0 ** -54, AL.mult, 2.0 ** -54, AL.mult)
    k0 = ts(new("cf", 1), kf, 0.0, AL.is_equal, -999.0, AL.mult)
    pm1 = ts(new("cf", 1), pf, -1.0, AL.add, k0, AL.add)
    shf = ts(new("cb", 128), col128, pm1, AL.is_equal, -1.0, AL.mult)
    DM = scaled(select(new("cb", 128), shf, [[-1, 128]], AL.not_equal, 1.0, 1), BIG / 2)
    k15 = ts(new("cf", 1), kf, 15.0, AL.is_equal, 1.5 * 2.0 ** 60, AL.mult)
    D15 = ts(new("cb", 128), ident, k15, AL.mult, 2.0 ** 60, AL.mult)
    BK = scaled(blk, kcol(EPS, 2 * EPS))
    BK1 = scaled(blk, kcol(EPS, 2 * EPS + 1))
    g15 = ts(new("cf", 1), g16, 15.0, AL.add)
    SEL = ts(new("cb", 144), col, g15, AL.is_equal)
    colk = ts(new("ti", 128), col128, 15, AL.bitwise_and)
    QK = tt(new("cb", 128), blk, ts(new("cb", 128), colk, 183.0, AL.add), AL.mult)
    offd = ts(new("cb", 128), colk, kf, AL.not_equal)
    DG1 = act(new("cb", 128), offd, AF.Identity, 0.0, -8192.0)
    DG2 = new("cb", 144)
    act(sub(DG2, 0, 128), offd, AF.Identity, -7.0 * 2 ** 17, -2.0 ** 23)
    fill(sub(DG2, 128, 143), -2.0 ** 23)
    fill(sub(DG2, 143, 144), 16384.0)
    B2k = scaled(blk, act(new("cf", 1), kf, AF.Exp, 0.0, LN2, None, 1300.0))
    first_exp = len(ops) - 2
    keep = new("cb", 512)
    fill(keep, 1.0)
    fill(sub(keep, 0, 512, 16), 0.0)
    for t in range(1, NV):
        fill(table(t)["z"], 0.0)
    ones32 = fill(new("cf", 128), 1.0)
    bi = ts(new("ti", 8), iota(new("ti", 8), [[16, 8]], ROT // 16, 0), kf, AL.add)
    bases = ts(new("cf", 8), ts(new("ti", 8), bi, 127, AL.bitwise_and), 16.0, AL.mult)

    def pl(t, d, n=1):
        return sub(t, d * HW, (d + n) * HW)
    tmp = {}

    def m(name, buf="tb", n=HW):
        if name not in tmp:
            tmp[name] = new(buf, n)
            names[(buf, tmp[name][1])] = name
        return tmp[name]

    def at(name, n=1):
        b, a = AT[name]
        names[("pb%d" % b, a * HW)] = name
        return tl("pb%d" % b, a * HW, (a + n) * HW)

    def state(t):
        j = min(t, 1)
        lb, li = tl("lb", j * 768, (j + 1) * 768), tl("li", j * 144, (j + 1) * 144)
        return {"EQ": pl(lb, 0, 4), "E": pl(lb, 0, 3), "Q": pl(lb, 3), "HP": pl(lb, 4, 2), "H": pl(lb, 4), "P0": pl(lb, 5),
                "li": sub(li, 0, HW + 9), "N": sub(li, 0, HW), "h2": sub(li, HW, HW + 9), "a7": sub(li, HW + 8, HW + 9)}

    def fixed(j):
        z = tl("ls", j * ST, (j + 1) * ST)
        return {"all": z, "dl": pl(z, 0, 3), "c0": pl(z, 3), "th": sub(z, 512, 513), "wt": sub(z, 513, 514), "pad": sub(z, 512, ST)}
    made = {}

    def derived(j):
        if j not in made:
            f = fixed(j)
            made[j] = (ts(new("tf", 1), f["th"], 2040.0 + 917504.5, AL.add), ts(new("tb", 128), blk, cp(new("tf", 1), f["wt"]), AL.mult))
        return made[j]

    def encode():
        s, f = state(0), fixed(0)
        ps, dv, ex = ps_in, dv_in, ex_in
        tt(s["Q"], ts(m("r"), ps, -1.0, AL.mult, kcol(1, -9), AL.add), ts(m("fp"), ps, 0.0, AL.is_lt, kcol(-1, 16), AL.mult), AL.add)
        vp = tt(m("u"), dv, ts(m("fu"), ps, 0.0, AL.is_lt, 4.0, AL.mult), AL.add)
        hm, e0 = m("tP", n=3 * HW), m("st", n=3 * HW)
        cd = act(m("eq", n=3 * HW), ex, AF.Identity, 2 * EPS, EPS)
        ops[-1]["deps"].add(first_exp)
        op = ts(m("gg", n=3 * HW), ex, -1.0, AL.is_equal, 2.0, AL.mult)
        for d in range(3):
            ts(pl(hm, d), vp, float(d), AL.is_equal)
            tt(pl(e0, d), sub(cd, d, 3 * HW, 3), sub(op, d, 3 * HW, 3), AL.max)
        nh = act(cd, hm, AF.Identity, 9.0, -10.0)
        tt(s["E"], e0, nh, AL.min)
        pr = tt(op, hm, e0, AL.mult)
        ph = at("enc")
        mm([(ph, I(), pl(pr, d)) for d in range(3)])
        act(s["H"], ph, AF.Identity)
        tt(s["N"], nm_in, act(m("sc", "tf"), dv, AF.Identity, float(ROT + 8192), -4096.0), AL.add)
        cs = [sub(dn_in, d, 3 * HW, 3) for d in range(3)]
        tt(pl(f["dl"], 0), cs[0], cs[1], AL.subtract)
        tt(pl(f["dl"], 1), cs[1], cs[2], AL.subtract)
        ts(pl(f["dl"], 2), cs[2], -2048.0, AL.add)
        ts(f["c0"], cs[0], -2048.0, AL.add)
        fill(f["pad"], 0.0)
        ts(f["th"], th_in, -2040.0, AL.add)
        cp(f["wt"], wt_in)
        send(f["all"], [fixed(j)["all"] for j in range(1, 4)], [-1, -2, -3], "fix")

    AQ = 0.61
    onS = PAR["onS"].split()

    def visit(t):
        s, X = state(t), table(t)
        j = (t - 1) % 4 if t else 0
        f = fixed(j)
        thp, BW = derived(j)
        Q, N, E, EQ = s["Q"], s["N"], s["E"], s["EQ"]
        if 0 < t < NV - 1:
            send(X["x"], table(t + 1)["x"], -1, "tab")
        r = act(m("r"), Q, AF.Exp, kcol(-AQ, AQ * (9 + 106)), AQ)
        p1 = at("p1")
        mm([(p1, IB, r)])
        fp = act(m("fp"), Q, AF.Relu, kcol(4, -32), -4.0)
        fu = act(m("fu"), Q, AF.Relu, -7.0)
        if "P" in onS:
            P = act(m("P"), p1, AF.Sign)
        else:
            P = ts(m("P"), p1, 0.0, AL.is_gt, 0.5, AL.subtract)
        px, pz = at("px", 2), at("pz")
        mm([(pl(px, 0), I(), fp), (pz, B(), fu)], True, False)
        mm([(pl(px, 0), I(), pl(E, d)) for d in range(3)], False, True)
        pc = tt(m("pc"), P, pl(px, 0), AL.is_gt)
        u = act(m("u"), Q, AF.Exp, kcol(AQ, -AQ * (9 + 113.5)), -AQ)
        tP = m("tP", n=3 * HW)
        for d in range(3):
            names[("tb", pl(tP, d)[1])] = "tP%d" % d
            tt(pl(tP, d), pl(E, d), pc, AL.mult)
        pm = at("pm", 3)
        mm([(pm, B(), tP)])
        st = act(m("st", n=3 * HW), pm, AF.Sign, kcol(-EPS, -1.5 * EPS))
        pcn = at("pcn")
        mm([(pcn, D15, one)] + [(pcn, DM, pl(st, d)) for d in range(3)])
        tw = tt(m("tw"), u, pcn, AL.min)
        p2 = at("p2")
        mm([(p2, TINY, P), (p2, IB, tw)])
        z = act(m("z", n=2 * HW), px, AF.Relu, 8.0, -512.0)
        pA = at("pA", 3)
        mm([(pl(pA, e, 3 - e), I(), pl(E, 0, 3 - e)) for e in range(3)], True, False)
        mm([(pl(pA, d), I(), pl(z, e)) for d in range(3) for e in range(2)], False, True)
        gg = act(m("gg", n=3 * HW), pA, AF.Sign, -0.5)
        pd = tt(m("pd", "th16", 3 * HW), gg, f["dl"], AL.mult)
        pcc = at("pcc")
        mm([(pcc, H16, f["c0"])] + [(pcc, H16, pl(pd, d)) for d in range(3)])
        nn = ts(m("nn", "ti"), N, 4095, AL.bitwise_and)
        Pp = ts(m("Pp%d" % t) if t else s["P0"], p2, 0.0, AL.is_gt)
        names[(Pp[0], Pp[1])] = "Pp"
        if t == 0:
            send(s["HP"], state(1)["HP"], 1, "seth")
        cnt = m("cnt", "tf", 1)
        if t < NV - 1:
            act(m("js"), p2, AF.Sign, -2.0e-32, 1.0, cnt)
        cP = tt(m("cP", "th16"), Pp, pcc, AL.mult)
        pcv = at("pcv")
        mm([(pcv, I(8192), fu), (pcv, IBm(8160.0, 2080.0), Pp), (pcv, B16, cP)])
        pct = at("pct")
        mm([(pct, I(), DG1), (pct, B(3232), Pp), (pct, B16, cP)])
        pr = m("pr", "ti", HW + 8)
        names[("ti", pr[1] + 8)] = "pre"
        tt(sub(pr, 8, HW + 8), nn, pcv, AL.mult)
        sc = scan(m("sc", "tf"), sub(keep, 0, HW), pct)
        ts(sub(pr, 0, 8), sub(sc, 15, HW, 16), 32.0, AL.mult)
        xi = ts(m("xi", "ti", HW + 8), pr, 5, AL.arith_shift_right, 2047 + (255 << 18), AL.bitwise_and)
        off = ts(m("off", "tu", HW + 8), xi, 2048.0, AL.min)
        xy, ad, ys = m("xy", n=17 * HW), m("ad", n=16 * HW), m("ys", n=16 * HW)
        xc, y = pl(xy, 0), pl(xy, 1, 16)
        for (e_, a, b) in PAR["gather"]:
            names[("tb", xy[1] + 16 * a)] = "y%d" % a
            gather(e_, sub(xy, 16 * a, 16 * b), X["g"], sub(off, a, b))
        kps = ts(m("kps"), cP, -0.5, AL.is_lt, 0.5, AL.subtract)
        pD = at("pD")
        mm([(pD, I(8192), fu), (pD, I(8192), Pp), (pD, B(-131072), kps)], True, False)
        for c in range(4):
            x, k0_ = c // 2, 8 * (c % 2)
            pdd = tl("pb%d" % (c % PAR["ring"]), 0, 512)
            names[(pdd[0], 0)] = "pdd%d" % c
            names[("tb", ad[1] + 512 * c)] = "ad%d" % c
            names[("tb", ys[1] + 512 * c)] = "ys%d" % c
            mm([(sub(pdd, 64 * k, 64 * k + 64), ident, sub(xc, 64 * x, 64 * x + 64)) for k in range(8)], True, False)
            mm([(sub(pdd, 64 * k, 64 * k + 64), I(-1), sub(y, 1024 * x + k0_ + k, 1024 * x + 1024, 16)) for k in range(8)], False, True)
            act(sub(ad, 512 * c, 512 * c + 512), pdd, AF.Abs)
            mm([(sub(pD, 64 * x, 64 * x + 64), sub(SEL, 15 - k0_ - k, 143 - k0_ - k), sub(ad, 512 * c + 64 * k, 512 * c + 64 * k + 64))
                for k in range(8)], False, c == 3)
            scan(sub(ys, 512 * c, 512 * c + 512), keep, sub(y, 512 * c, 512 * c + 512))
        ts(Q, Q, 8.0, AL.min)
        pt2 = at("pt2")
        mm([(pt2, I(), tw), (pt2, I(-BIG), Pp)])
        t2 = act(m("t2"), pt2, AF.Relu)
        p3 = at("p3")
        mm([(p3, IB, t2)])
        if "J2" in onS:
            j2, jm, jb = act(m("J2"), p3, AF.Sign, -2.0 ** -110), scaled(BK, 0.5), 0.59375
        else:
            j2, jm, jb = ts(m("J2"), p3, 0.0, AL.is_gt), BK, 0.0
        pR = at("pR", 3)
        mm([(pl(pR, d), BK, Pp) for d in range(3)])
        eq = tt(m("eq", n=3 * HW), E, pR, AL.is_equal)
        pcm = at("pcm")
        mm([(pcm, I(), pl(z, 0)), (pcm, I(), pl(z, 1)), (pcm, I(16), Pp), (pcm, jm, j2)])
        cm = act(m("cm"), pcm, AF.Identity, -17.0 + jb)
        prs = at("prs", 4)
        pe3, pq = pl(prs, 0, 3), pl(prs, 3)
        mm([(pe3, I(-1), E), (pq, I(), fu), (pq, I(-8 if "P" in onS else -16), P), (pq, IBm(512.0, -496.0), Pp)], True, False)
        mm([(pe3, I(256), eq)], False, False)
        mm([(pl(pe3, d), I(), cm) for d in range(3)], False, True)
        tt(EQ, EQ, prs, AL.max)
        pup = at("pup")
        mm([(pup, I(), u), (pup, I(-BIG), Pp)])
        up = act(m("up"), pup, AF.Relu)
        pY = at("pY")
        mm([(pY, IB, up)])
        if "nq" in onS:
            pn = at("pn")
            mm([(pn, I(), fp), (pn, I(2048), act(m("Yh"), pY, AF.Sign))])
            nq = act(m("nq"), pn, AF.Relu, -512.0, 0.25)
        else:
            nq = tt(m("nq"), ts(m("Yh"), pY, 0.0, AL.is_gt, 0.25, AL.mult), fp, AL.mult)
        U, UQ = at("U", 3), at("UQ")
        ub = [pl(U, i) for i in range(3)]
        mm([(U, I(-8), gg), (pl(U, 1, 2), I(8), pl(gg, 0, 2))], True, False)
        mm([(ub[0], IBm(-16.0, 23.0), Pp), (ub[1], IBm(-16.0, 31.0), Pp), (ub[2], IBm(-16.0, 31.0), Pp)], False, False)
        mm([(UQ, QK, Pp), (UQ, I(-384), kps), (UQ, B(-1), nq)], True, False)
        thr = ts(m("thr", "tf", 1), s["a7"], 16.0, AL.mult, thp, AL.add) if t else thp
        cf = ts(m("cf"), pD, thr, AL.is_le, 131072.0, AL.mult)
        mm([(UQ, B(), cf)], False, True)
        tt(Q, Q, UQ, AL.min)
        if t == 0:
            send(Q, state(1)["Q"], 1, "setq")
        tO = tt(m("tO"), cf, r, AL.mult)
        p4 = at("p4")
        mm([(p4, IB, tO)])
        O = ts(m("O"), p4, 0.0, AL.is_gt)
        mm([(ub[0], BK1, O), (ub[1], BK1, O), (ub[2], BK1, O)], False, True)
        tt(E, E, U, AL.min)
        pN = at("pN")
        mm([(pN, I16, cP), (pN, I(2048), pl(gg, 0)), (pN, I(2048), pl(gg, 1)), (pN, I(7328), Pp), (pN, I(32768 * (t + 1)), kps),
            (pN, B(-1), cf)])
        tt(N, N, pN, AL.max)
        if t == 0:
            send(E, state(1)["E"], 1, "sete")
        Y = sub(ys, 15, 16 * HW, 16)
        msg = tl("mo", 144 * t, 144 * t + HW + 8)
        pv = at("pv")
        mm([(pv, I(0.5), xc), (pv, I(0.5), Y)])
        ts(sub(msg, 0, HW), pv, -0.25, AL.add)
        ns = 9 if t < NV - 1 else 8
        ph = sub(at("ph", 2), 0, 16 * ns)
        mm([(ph, I(), sub(DG2, 0, 16 * ns))] + ([(sub(ph, 143, 144), ones32, cnt)] if ns == 9 else [])
           + [(pl(ph, 0), B(-131072), kps), (pl(ph, 0), BW, Y), (pl(ph, 0), B(), cf)])
        sh = scan(sub(m("sh", "tf", 144), 0, 16 * ns), sub(keep, 0, 16 * ns), ph)
        h1 = cp(sub(m("h1", "ti", 9), 0, ns), sub(sh, 15, 16 * ns, 16))
        h2 = ts(sub(s["h2"], 0, ns), h1, (31 << 17) + 15, AL.bitwise_and)
        h3 = ts(m("h3", "tf", 8), sub(h2, 0, 8), 2064.0, AL.min)
        cp(sub(msg, HW, HW + 8), tt(m("h4", "tf", 8), h3, bases, AL.add))
        if t == 0:
            send(s["li"], state(1)["li"], 1, "seti")
        if 0 < t < NV - 1:
            land = tl("mi", 144 * t, 144 * t + HW + 8)
            send(msg, land, -1, "new")
            scatter(table(t + 1)["w"], land)
        else:
            scatter(X["w"], msg)

    def decode():
        s = state(NV - 1)
        ts(tl("of", 0, HW), ts(m("nn", "ti"), s["N"], 4095, AL.bitwise_and), -float(ROT), AL.add)
        ts(tl("ob", 128, 256), ts(m("n2", "ti"), s["N"], 12, AL.arith_shift_right, 3, AL.bitwise_and), -1.0, AL.mult, 2.0, AL.add)
        tt(tl("ob", 0, HW), ts(m("r"), s["Q"], -1.0, AL.mult, kcol(1, -9), AL.add),
           ts(m("u"), s["Q"], 16.0, AL.is_le, 2.0, AL.subtract), AL.max)
        pe, pM, pH = at("pe"), at("pM"), at("pH")
        mm([(pe, I(), s["P0"])] + [(pe, I(), m("Pp%d" % t)) for t in range(1, NV)])
        ev = ts(m("ev"), pe, 0.0, AL.is_gt)
        mm([(pM, B2k, ev)])
        fx = tt(m("fx"), act(m("f1"), s["H"], AF.Exp, 17 * LN2, -128 * LN2), ts(m("f2"), s["H"], 2.0 ** 22, AL.mult), AL.min)
        bit = ts(m("b2", "ti"), tt(m("b1", "ti"), fx, pM, AL.mult), 15, AL.arith_shift_right, 1, AL.bitwise_and)
        mm([(pH, I(), s["H"]), (pH, I(), ev), (pH, I(), cp(m("b3"), bit))])
        H = act(m("H"), pH, AF.Identity)
        pw = at("pw", 3)
        mm([(pw, I(-8), ones), (pw, I(-8), s["E"])] + [(pl(pw, d), I(), H) for d in range(3)])
        e1 = tt(m("tP", n=3 * HW), s["E"], pw, AL.max)
        xx = ts(m("st", n=3 * HW), e1, 1.0, AL.min, 128.0, AL.mult)
        sg = act(m("gg", n=3 * HW), e1, AF.Sign, -0.5)
        po = at("po", 3)
        mm([(po, I(), xx), (po, I(-63.5), sg)])
        for d in range(3):
            act(tl("ob", 256 + d, 640, 3), pl(po, d), AF.Identity, -65.5)

    phase[0] = 0
    encode()
    for t in range(NV):
        phase[0] = 0 if t == 0 else (2 if t == NV - 1 else 1)
        visit(t)
    decode()
    b = table(NV - 1)["x"]
    dma("Y", tl("yx", 0, 2048 - ROT), sub(b, ROT, 2048))
    dma("S", tl("yx", 2048 - ROT, 2048), sub(b, 0, ROT))
    dma("Y", tl("yn", 0, 128), tl("of", 0, 128))
    dma("Y", tl("yp", 0, 128), tl("ob", 0, 128))
    dma("Y", tl("yd", 0, 128), tl("ob", 128, 256))
    dma("Y", tl("yg", 0, 384), tl("ob", 256, 640))
    assert narr[0] == NARR
    return ops


def schedule(ops, shift):
    n = len(ops)
    lat = [o["cost"] + (PAR["dma"] if o["kind"] == "dma" else 0.0) for o in ops]
    succ = [[] for _ in ops]
    for i, o in enumerate(ops):
        for j in o["deps"]:
            succ[j].append(i)
    prio = [0.0] * n
    for i in range(n - 1, -1, -1):
        prio[i] = lat[i] + max([prio[j] + PAR["cross"] for j in succ[i]] + [0.0])
    rank_ = [prio[i] + shift.get(o["role"], 0.0) for i, o in enumerate(ops)]
    for i in range(n - 1, -1, -1):
        if ops[i]["const"] and succ[i]:
            rank_[i] = lat[i] + PAR["cross"] + max(rank_[j] for j in succ[i]) + shift.get(ops[i]["role"], 0.0)
    left = [len(o["deps"]) for o in ops]
    ready = [i for i in range(n) if not left[i]]
    fin = [0.0] * n
    base = [0.0] * n
    free = {}
    lastb = {}
    held = {}
    order = []
    while ready:
        cand = []
        for i in ready:
            o = ops[i]
            if o["kind"] == "mm" and o["args"][1] and any(held.get(b) for b in o["banks"]):
                continue
            st = max(base[i], free.get(o["eng"], 0.0) if o["eng"] else 0.0)
            for b in o["banks"]:
                for e, j in lastb.get(b, {}).items():
                    if e != o["eng"]:
                        st = max(st, fin[j] + PAR["cross"])
            cand.append((st, i))
        t0, i0 = min(cand, key=lambda c: c[0] + PAR["look"] * ops[c[1]]["cost"])
        t0 += PAR["look"] * ops[i0]["cost"]
        st, i = max([c for c in cand if c[0] <= t0 and ops[c[1]]["eng"] == ops[i0]["eng"]],
                    key=lambda c: rank_[c[1]])
        o = ops[i]
        o["waits"] = set(o["deps"])
        for b in o["banks"]:
            for e, j in lastb.get(b, {}).items():
                if e != o["eng"]:
                    o["waits"].add(j)
            lastb.setdefault(b, {})[o["eng"]] = i
            if o["kind"] == "mm":
                held[b] = not o["args"][2]
        fin[i] = st + lat[i]
        if o["eng"]:
            free[o["eng"]] = st + o["cost"]
        o["start"], o["prio"] = st, prio[i]
        order.append(i)
        ready.remove(i)
        for j in succ[i]:
            d = 0.0 if (o["eng"] == "P" and ops[j]["eng"] == "P") else (PAR["same"] if ops[j]["eng"] == o["eng"] else PAR["cross"])
            base[j] = max(base[j], fin[i] + d)
            left[j] -= 1
            if not left[j]:
                ready.append(j)
    assert len(order) == n
    return order, max(fin)


def search(ops):
    roles = sorted(set(o["role"] for o in ops))
    seed = [PAR["seed"]]

    def rnd():
        seed[0] = (seed[0] * 1103515245 + 12345) % 2147483648
        return seed[0] / 2147483648.0

    def delays(order):
        prev, last = {}, {}
        fin = {i: ops[i]["start"] + ops[i]["cost"] + (PAR["dma"] if ops[i]["kind"] == "dma" else 0.0) for i in order}
        for i in order:
            if ops[i]["eng"]:
                prev[i] = last.get(ops[i]["eng"])
                last[ops[i]["eng"]] = i
        i = max(order, key=lambda j: fin[j])
        out = []
        while True:
            c = [(fin[j], j) for j in ops[i]["waits"]]
            if prev.get(i) is not None:
                c.append((ops[prev[i]]["start"] + ops[prev[i]]["cost"] - 60.0, prev[i]))
            if not c:
                return out
            j = max(c)[1]
            if j not in ops[i]["deps"]:
                out.append((i, j))
            i = j
    shift = {}
    order, cur = schedule(ops, shift)
    best, kept, q = cur, {}, delays(order)
    for it in range(PAR["iters"]):
        tr = dict(shift)
        for _k in range(1 + int(rnd() * 2.5)):
            if rnd() < 0.7 and q:
                i, j = q[int(rnd() * len(q))]
                r, sg = (ops[i]["role"], 1.0) if rnd() < 0.5 else (ops[j]["role"], -1.0)
                tr[r] = tr.get(r, 0.0) + sg * rnd() * PAR["step"]
            else:
                r = roles[int(rnd() * len(roles))]
                tr[r] = tr.get(r, 0.0) + (rnd() - 0.5) * 2 * PAR["step"]
        order, v = schedule(ops, tr)
        if v <= cur + 400.0 * (1.0 - it / PAR["iters"]) * rnd():
            cur, shift, q = v, tr, delays(order)
            if v < best:
                best, kept = v, tr
    return schedule(ops, kept)


def place(ops, pred, low, prio):
    n = len(ops)
    succ = [[] for _ in ops]
    left = [len(pred[i]) for i in range(n)]
    for i in range(n):
        for j, _w in pred[i]:
            succ[j].append(i)
    heap = sorted((-prio[i], i) for i in range(n) if not left[i])
    start = [0.0] * n
    busy = {}
    gap = PAR["cross"]
    while heap:
        i = heap.pop(0)[1]
        o = ops[i]
        t = max([low[i]] + [start[j] + w for j, w in pred[i]])
        c, e = o["cost"], o["eng"]
        res = [(e, 0.0)] + [(b, gap) for b in o["banks"]] if e else []
        moved = True
        while moved:
            moved = False
            for r, g_ in res:
                lst = busy.get(r, ())
                k = len(lst) - 1
                while k >= 0 and lst[k][0] > t - 2500.0:
                    k -= 1
                for a, b, e2 in lst[k + 1:]:
                    if a - g_ >= t + c:
                        break
                    if b + g_ > t and (g_ == 0.0 or e2 != e):
                        t = b + g_
                        moved = True
        start[i] = t
        for r, _g in res:
            lst = busy.setdefault(r, [])
            k = len(lst)
            while k and lst[k - 1][0] > t:
                k -= 1
            lst.insert(k, (t, t + c, e))
        for j in succ[i]:
            left[j] -= 1
            if not left[j]:
                k = len(heap)
                while k and heap[k - 1][0] > -prio[j]:
                    k -= 1
                heap.insert(k, (-prio[j], j))
    return start


def search(ops):
    n = len(ops)
    cost = [o["cost"] for o in ops]
    lat = [o["cost"] + (PAR["dma"] if o["kind"] == "dma" else 0.0) for o in ops]
    fwd, bwd = [[] for _ in ops], [[] for _ in ops]
    for i, o in enumerate(ops):
        for j in o["deps"]:
            e = ops[j]["eng"]
            w = lat[j] + (0.0 if e == o["eng"] == "P" else PAR["same"] if e == o["eng"] else PAR["cross"])
            fwd[i].append((j, w))
            bwd[j].append((i, w + cost[i] - cost[j]))
    zero, tail = [0.0] * n, [lat[i] - cost[i] for i in range(n)]
    seed = [PAR["seed"]]

    def rnd():
        seed[0] = (seed[0] * 1103515245 + 12345) % 2147483648
        return seed[0] / 2147483648.0
    prio = [0.0] * n
    for i in range(n - 1, -1, -1):
        prio[i] = max([tail[i]] + [prio[j] + w for j, w in bwd[i]])
    prio = [prio[i] + cost[i] for i in range(n)]
    best, cur = None, None
    for it in range(PAR["iters"]):
        s = place(ops, fwd, zero, prio)
        r = place(ops, bwd, tail, [s[i] + cost[i] for i in range(n)])
        back = [r[i] + cost[i] for i in range(n)]
        s = place(ops, fwd, zero, back)
        v = max(s[i] + lat[i] for i in range(n))
        if best is None or v < best[0]:
            best = (v, s)
        if cur is None or v <= cur[0] + PAR["slack"] * rnd() * (1.0 - it / PAR["iters"]):
            cur = (v, back)
        shake = {}
        prio = [cur[1][i] + shake.setdefault(ops[i]["role"], (rnd() - 0.5) * PAR["step"] if rnd() < PAR["share"] else 0.0) for i in range(n)]
    order = sorted(range(n), key=lambda i: (best[1][i], i))
    last = {}
    for i in order:
        o = ops[i]
        o["start"] = best[1][i]
        o["waits"] = set(o["deps"])
        for b in o["banks"]:
            o["waits"].update(j for e, j in last.get(b, {}).items() if e != o["eng"])
            last.setdefault(b, {})[o["eng"]] = i
    return order, best[0]


PLAN = {}


def rank_program(g, core, T, topo):
    rank = T.rank_of(core)
    if rank is None:
        return
    if not PLAN:
        PLAN["ops"] = build()
        PLAN["order"] = search(PLAN["ops"])[0]
    ops, order = PLAN["ops"], PLAN["order"]
    queue = {"V": g.vector, "S": g.scalar, "P": g.tensor, "G": g, "Y": g.sync}
    count = {}
    token = {}
    clock = {}
    known = {k: {} for k in queue}
    ndma = [0]

    def peer(hop):
        return T.cores[(rank + hop) % len(T.cores)]

    def ap(t):
        if not isinstance(t, tuple):
            return t
        if t[0] not in SCRATCH and t[1] == 0 and t[2] == T[t[0]].shape[1]:
            return T[t[0]][:]
        if t[3] == 1:
            return T[t[0]][0:t[4], t[1]:t[2]]
        return T[t[0]][0:t[4], t[1]:t[2]:t[3]]

    def win(w, off):
        return T[w[0]][:, w[1]:w[2]].indirect(T[off[0]][:, off[1]:off[2]])

    for i in order:
        o = ops[i]
        e, kind, a = o["eng"], o["kind"], o["args"]
        if kind == "recv":
            n = sum(len(topo.engines(peer(-h), core)) for h in ops[a[1]]["args"][3])
            token[i] = ("arr%d" % a[0], n)
            count[token[i][0]] = n
            clock[i] = {token[i][0]: n}
            continue
        q, kn = queue[e], known[e]
        need = {}
        for j in o["waits"]:
            if (e == "P" and ops[j]["eng"] == "P") or ops[j]["kind"] == "send":
                continue
            s_, v = token[j]
            if v > need.get(s_, (0, 0))[0]:
                need[s_] = (v, j)
        for s_, (v, j) in sorted(need.items(), key=lambda z: -ops[z[1][1]]["start"]):
            if kn.get(s_, 0) < v:
                q.wait_ge(T.sem[s_], v)
                for k_, v_ in clock[j].items():
                    kn[k_] = max(kn.get(k_, 0), v_)
        if kind == "send":
            dst = peer(a[3][0])
            to = [topo.addr(peer(h), core) for h in a[3]]
            if len(to) == 1:
                g.remote_dma(ap(a[1][0]), ap(a[0]), T.sem["arr%d" % a[2]], T.sem.sent, to[0][1], to[0][0], topo.mask(core, dst))
            else:
                g.remote_dma_fused([RemoteDMATransfer(dst_ids=[DstId(rid=r_, pnc=p_) for r_, p_ in to], dma_engine_mask=topo.mask(core, dst),
                                                      remote_sem=T.sem["arr%d" % a[2]], srcs=[ap(a[0])], dsts=[ap(d_) for d_ in a[1]])],
                                   local_sem=T.sem.sent)
            count["sent"] = count.get("sent", 0) + len(topo.engines(core, dst))
            continue
        if kind == "ts":
            if a[5] is None:
                ins = q.tensor_scalar(ap(a[0]), ap(a[1]), ap(a[2]), None, a[4])
            else:
                ins = q.tensor_scalar(ap(a[0]), ap(a[1]), ap(a[2]), ap(a[3]), a[4], a[5])
        elif kind == "tt":
            ins = q.tensor_tensor(ap(a[0]), ap(a[1]), ap(a[2]), a[3])
        elif kind == "cp":
            ins = q.tensor_copy(ap(a[0]), ap(a[1]))
        elif kind == "fill":
            ins = q.memset(ap(a[0]), int(a[1]) if SCRATCH[a[0][0]][2] == "int32" else a[1])
        elif kind == "scan":
            ins = q.tensor_tensor_scan(ap(a[0]), ap(a[1]), ap(a[2]), 0.0, AL.mult, AL.max)
        elif kind == "act":
            ins = q.activation(ap(a[0]), ap(a[1]), a[2], bias=ap(a[3]), scale=ap(a[4]), accum_out=ap(a[5]))
        elif kind == "gat":
            if e == "S":
                ins = q.activation(ap(a[0]), win(a[1], a[2]), AF.Identity)
            else:
                ins = q.tensor_copy(ap(a[0]), win(a[1], a[2]))
        elif kind == "sca":
            ins = q.tensor_copy(win(a[0], a[1]), ap(a[2]))
        elif kind == "mm":
            for k_, (o_, l_, r_) in enumerate(a[0]):
                ins = q.matmul(ap(o_), ap(l_), ap(r_), a[1] and k_ == 0, a[2] and k_ == len(a[0]) - 1)
        elif kind == "iota":
            ins = g.iota(ap(a[0]), a[1], a[2], a[3])
        elif kind == "sel":
            ins = g.affine_select(ap(a[0]), ap(a[1]), a[2], a[3], a[4], 0, a[5])
        elif kind == "dma":
            ins = q.dma_start(ap(a[0]), ap(a[1]))
        if kind == "dma":
            s_, inc = "dma%d" % ndma[0], 16
            ndma[0] += 1
        else:
            s_, inc = "q" + e, 1
        ins.then_inc(T.sem[s_], inc)
        count[s_] = count.get(s_, 0) + inc
        token[i] = (s_, count[s_])
        clock[i] = dict(kn)
        clock[i][s_] = count[s_]
    for s_, v in count.items():
        g.wait_ge(T.sem[s_], v)
